import numpy as np
import ml_dtypes


def mxq(x, axis, fmt="e4m3"):
    dtype, down = {"e4m3": (ml_dtypes.float8_e4m3fn, 7), "e5m2": (ml_dtypes.float8_e5m2, 14)}[fmt]
    v = np.moveaxis(np.asarray(x, np.float32).astype(ml_dtypes.bfloat16).astype(np.float64), axis, -1)
    blocks = v.reshape(v.shape[:-1] + (-1, 32))
    amax = np.abs(blocks).max(-1, keepdims=True)
    byte = np.maximum(np.where(amax > 0, np.frexp(amax)[1] - 1 + 127, 0) - down, 1)
    scale = np.exp2(byte - 127.0)
    codes = (blocks / scale).astype(np.float32).astype(dtype).astype(np.float64)
    return np.moveaxis((codes * scale).reshape(v.shape), -1, axis)


WIDE = False


def mx_kscale(k):
    if not WIDE:
        return np.ones(k)
    levels = np.array([10, -10, 5, -5, 0])
    if k % 512:
        return np.exp2(np.random.permutation(np.resize(levels, k // 32))).repeat(32)
    a = np.empty((k // 512, 16))
    for p in range(k // 512):
        a[p, :8] = np.random.permutation(np.resize(levels, 8))
        for g in range(8):
            far = levels[np.abs(levels - a[p, g]) >= 10]
            a[p, g + 8] = far[np.random.randint(len(far))]
    return np.exp2(a.ravel()).repeat(32)


BF16 = ml_dtypes.bfloat16


def bf(x):
    return np.asarray(x, np.float32).astype(BF16)


def f64(x):
    return np.asarray(x).astype(np.float64)


E2M1 = np.array([0.0, 0.5, 1.0, 1.5, 2.0, 3.0, 4.0, 6.0, -0.0, -0.5, -1.0, -1.5, -2.0, -3.0, -4.0, -6.0])


def pack_weight(w, fmt):
    k, n = w.shape
    w = f64(bf(w)).reshape(k // 32, 32, n)
    amax = np.abs(w).max(1)
    if fmt == "e4m3":
        byte = np.frexp(amax)[1] - 1 + 127 - 7
    else:
        mant, ex = np.frexp(amax / 6.0)
        byte = np.where(mant > 0.5, ex, ex - 1) + 127
    byte = np.clip(np.where(amax > 0, byte, 1), 1, 254)
    scaled = (w * np.exp2(127.0 - byte)[:, None, :]).reshape(k, n).astype(np.float32)
    by_word = np.ascontiguousarray(scaled.reshape(k // 512, 128, 4, n).transpose(0, 1, 3, 2))
    if fmt == "e4m3":
        words = by_word.astype(ml_dtypes.float8_e4m3fn).view(np.uint8)
    else:
        c = by_word.astype(ml_dtypes.float4_e2m1fn).view(np.uint8) & 0xF
        words = c[..., 0::2] | (c[..., 1::2] << 4)
    return np.ascontiguousarray(words), np.ascontiguousarray(byte.astype(np.uint8).reshape(k // 512, 16, n))


def unpack_weight(words, scales, fmt):
    g, p, n, _ = words.shape
    if fmt == "e4m3":
        vals = np.ascontiguousarray(words).view(ml_dtypes.float8_e4m3fn).astype(np.float64)
    else:
        nib = np.empty((g, p, n, 4), np.uint8)
        nib[..., 0::2] = words & 0xF
        nib[..., 1::2] = words >> 4
        vals = E2M1[nib]
    vals = vals * np.repeat(np.exp2(scales.astype(np.float64) - 127.0), 8, axis=1)[..., None]
    return vals.transpose(0, 1, 3, 2).reshape(g * 512, n)
def pack4(w):
    words, scales = pack_weight(w, "e2m1")
    return words.reshape(words.shape[0], 128, -1), scales


def unpack4(words, scales):
    return unpack_weight(words.reshape(words.shape[0], 128, -1, 2), scales, "e2m1")


def planes(Y):
    n, m = Y.shape
    b = f64(bf(Y)).reshape(n // 32, 32, m)
    amax = np.abs(b).max(1)
    byte = np.clip(np.where(amax > 0, np.frexp(amax)[1] - 1 + 127 - 7, 1), 1, 254)
    codes = (b * np.exp2(127.0 - byte)[:, None, :]).reshape(n, m).astype(np.float32).astype(ml_dtypes.float8_e4m3fn).view(np.uint8)
    words = codes.reshape(n // 512, 128, 4, m).transpose(0, 1, 3, 2)
    return np.ascontiguousarray(words), np.ascontiguousarray(byte.astype(np.uint8).reshape(n // 512, 16, m))


T, K, F, S = 2048, 1536, 1024, 512


def setup_inputs():
    s = mx_kscale(K)
    t = mx_kscale(F)
    potential = 2.5 * np.random.randn(K, T)
    R = 1.0 / (1.0 + np.exp(-potential)) - 0.5
    C = 4.0 * np.random.randn(K, F) / np.sqrt(K)
    rate_words, rate_scales = pack4(R * s[:, None])
    conn_words, conn_scales = pack4(C / s[:, None])
    gain = bf(np.exp(0.4 * np.random.randn(F)) * t)
    lead = bf(2.0 * np.random.randn(F, S) / np.sqrt(F) / t[:, None])
    background = bf(0.4 * np.random.randn(T, S))
    calib = bf(np.exp(0.8 * np.random.randn(S)))
    return {"rate_words": rate_words, "rate_scales": rate_scales, "conn_words": conn_words, "conn_scales": conn_scales,
            "gain": gain, "lead": lead, "background": background, "calib": calib}


def reference(rate_words, rate_scales, conn_words, conn_scales, gain, lead, background, calib):
    R = unpack4(rate_words, rate_scales)
    C = unpack4(conn_words, conn_scales)
    U = R.T @ C
    P = f64(gain)[None, :] * (1.0 / (1.0 + np.exp(-U)))
    E = mxq(P, 1, "e4m3") @ mxq(f64(lead), 0, "e4m3")
    y = (E + f64(background)) * f64(calib)[None, :]
    words, scales = planes(y.T)
    return y, words, scales

@@ -1,0 +1,383 @@
+from contextlib import ExitStack
+
+import concourse.mybir as mybir
+from concourse.masks import make_identity
+
+T, K, F, S = 2048, 1536, 1024, 512
+FLOPS = 2 * T * K * F + 2 * T * F * S
+
+F32 = mybir.dt.float32
+BF16 = mybir.dt.bfloat16
+I32 = mybir.dt.int32
+U8 = mybir.dt.uint8
+FP4X4 = mybir.dt.float4_e2m1fn_x4
+FP8X4 = mybir.dt.float8_e4m3fn_x4
+ACT = mybir.ActivationFunctionType
+ALU = mybir.AluOpType
+
+P = 128
+PACK = 4
+K_PASS = P * PACK
+KP = K // K_PASS
+FG = F // K_PASS
+BANK = 512
+CHUNKS = [256] * 7 + [128] * 2
+RATE_LOADS = [256, 256, 512, 1024]
+RATE_SCALE_LOADS = [512, 1536]
+BG_LOADS = [512, 512, 1024]
+CODE_STORES = [512, 1024, 1536, 1792, 1920, 2048]
+SCALE_STORES = [1792, 2048]
+WARM_PASSES = 20
+
+
+def starts(widths):
+    return [sum(widths[:i]) for i in range(len(widths))]
+
+
+def locate(widths, t0):
+    first = starts(widths)
+    i = max(j for j in range(len(widths)) if first[j] <= t0)
+    return i, t0 - first[i]
+
+
+def tile_neural_mass_eeg_k5_kernel(
+    tc, rate_words, rate_scales, conn_words, conn_scales, gain, lead, background, calib, out_0, out_1, out_2
+):
+    nc = tc.nc
+    with ExitStack() as ctx:
+        keep = ctx.enter_context(tc.tile_pool(name="keep", bufs=1))
+        work = ctx.enter_context(tc.tile_pool(name="work", bufs=3))
+        psum = ctx.enter_context(tc.psum_pool(name="psum", bufs=2))
+        ctx.enter_context(tc.manual_schedule())
+
+        def kept(name, shape, dtype):
+            return keep.tile(shape, dtype, name=name, align_bytes=64)
+
+        conn_raw = [kept("conn_raw%d" % g, [P, KP, 2 * K_PASS], U8) for g in range(FG)]
+        conn_sc_raw = kept("conn_sc_raw", [P, KP, F], U8)
+        conn_w = [kept("conn_w%d" % g, [P, PACK, KP, 2 * P], U8) for g in range(FG)]
+        conn_sc = [kept("conn_sc%d" % g, [P, PACK, KP, P], U8) for g in range(FG)]
+        rate_w = [kept("rate_w%d" % i, [P, KP, 2 * w], U8) for i, w in enumerate(RATE_LOADS)]
+        rate_sc = [kept("rate_sc%d" % i, [P, KP, w], U8) for i, w in enumerate(RATE_SCALE_LOADS)]
+        lead_raw = [kept("lead_raw%d" % g, [P, PACK, S], BF16) for g in range(FG)]
+        lead_il = [kept("lead_il%d" % g, [P, S, PACK], BF16) for g in range(FG)]
+        lead_w = [kept("lead_w%d" % g, [P, PACK * S], U8) for g in range(FG)]
+        lead_sc = [kept("lead_sc%d" % g, [P, S], U8) for g in range(FG)]
+        bg = [kept("bg%d" % i, [P, w // P, S], BF16) for i, w in enumerate(BG_LOADS)]
+        calib_all = kept("calib_all", [P, S], BF16)
+        gain_rows = kept("gain_rows", [PACK, FG * P], BF16)
+        gain_sq = kept("gain_sq", [P, FG * P], F32)
+        gain_ps = psum.tile([P, FG, P], F32, name="gain_ps", tag="gain_ps", bufs=1)
+        zero_bf = kept("zero_bf", [P, K_PASS], BF16)
+        zero_w = kept("zero_w", [P, K_PASS], U8)
+        zero_sc = kept("zero_sc", [P, P], U8)
+        ident = kept("ident", [P, P], F32)
+        warm = kept("warm", [P, 1], F32)
+        y_w = kept("y_w", [P, PACK * T], U8)
+        y_sc = kept("y_sc", [P, T], U8)
+
+        rate_words32 = rate_words.bitcast(I32)
+        conn_words32 = conn_words.bitcast(I32)
+        rate_scales32 = rate_scales.bitcast(I32)
+        conn_scales32 = conn_scales.bitcast(I32)
+
+        def load_conn_words(g):
+            nc.gpsimd.dma_start(
+                out=conn_raw[g][:].bitcast(I32),
+                in_=conn_words32[:, :, 256 * g : 256 * (g + 1)].rearrange("k p c -> p k c"),
+            )
+
+        def load_rate_words(i, queue):
+            t0 = starts(RATE_LOADS)[i]
+            queue.dma_start(
+                out=rate_w[i][:].bitcast(I32),
+                in_=rate_words32[:, :, t0 // 2 : (t0 + RATE_LOADS[i]) // 2].rearrange("k p c -> p k c"),
+            )
+
+        def load_rate_scales(i):
+            t0 = starts(RATE_SCALE_LOADS)[i]
+            for q in range(4):
+                nc.sync.dma_start(
+                    out=rate_sc[i][32 * q : 32 * q + 4].bitcast(I32),
+                    in_=rate_scales32[:, 4 * q : 4 * q + 4, t0 // 4 : (t0 + RATE_SCALE_LOADS[i]) // 4].rearrange(
+                        "k r c -> r k c"
+                    ),
+                )
+
+        def load_conn_scales():
+            for q in range(4):
+                nc.scalar.dma_start(
+                    out=conn_sc_raw[32 * q : 32 * q + 4].bitcast(I32),
+                    in_=conn_scales32[:, 4 * q : 4 * q + 4, :].rearrange("k r c -> r k c"),
+                )
+
+        def load_lead(g):
+            rows = lead[K_PASS * g : K_PASS * (g + 1), :].rearrange("(q t r) s -> r q t s", t=PACK, r=4)
+            for r in range(4):
+                nc.sync.dma_start(out=lead_raw[g][r:P:4], in_=rows[r])
+
+        def load_gain():
+            nc.gpsimd.dma_start(
+                out=gain_rows[:].rearrange("t (q r) -> t q r", r=4),
+                in_=gain.rearrange("(q t r) -> t q r", t=PACK, r=4),
+            )
+
+        def load_bg(i):
+            t0 = starts(BG_LOADS)[i]
+            nc.sync.dma_start(out=bg[i][:], in_=background[t0 : t0 + BG_LOADS[i], :].rearrange("(a p) s -> p a s", p=P))
+
+        def permute_conn(g, t0, t1):
+            n = t1 - t0
+            nc.vector.tensor_copy(
+                out=conn_w[g][:, t0:t1].rearrange("p t k c -> p (t k c)").bitcast(I32).rearrange("p (t m w) -> p t m w", t=n, w=2),
+                in_=conn_raw[g][:].rearrange("p k c -> p (k c)").bitcast(I32).rearrange("p (m t w) -> p t m w", t=PACK, w=2)[:, t0:t1],
+            )
+            nc.vector.tensor_copy(
+                out=conn_sc[g][:, t0:t1].rearrange("p t k c -> p (t k c)").bitcast(I32).rearrange("p (t k m) -> p t k m", t=n, k=KP),
+                in_=conn_sc_raw[:].bitcast(I32)[:, :, P * g : P * (g + 1)].rearrange("p k (m t) -> p t k m", t=PACK)[:, t0:t1],
+            )
+
+        def interleave_lead(g):
+            nc.vector.tensor_copy(
+                out=lead_il[g][:].rearrange("p (c i) t -> p c t i", i=4),
+                in_=lead_raw[g][:].rearrange("p t (c i) -> p c t i", i=4),
+            )
+
+        def quantize_lead(g):
+            nc.vector.quantize_mx(
+                out=lead_w[g][:].bitcast(FP8X4), scales=lead_sc[g][:], in_=lead_il[g][:].rearrange("p s t -> p (s t)")
+            )
+
+        load_conn_words(0)
+        load_rate_words(0, nc.gpsimd)
+        load_conn_words(1)
+        load_gain()
+        make_identity(nc, ident[:])
+
+        nc.vector.memset(conn_sc_raw[:].rearrange("p k c -> p (k c)").bitcast(I32), 0)
+        nc.vector.memset(rate_sc[0][:].rearrange("p k c -> p (k c)").bitcast(I32), 0)
+        nc.vector.memset(zero_bf[:], 0.0)
+        nc.vector.memset(warm[:], 0.0)
+        nc.vector.quantize_mx(out=zero_w[:].bitcast(FP8X4), scales=zero_sc[:], in_=zero_bf[:])
+        load_rate_scales(0)
+        load_conn_scales()
+        nc.scalar.activation(out=warm[:], in_=warm[:], func=ACT.Sigmoid)
+        warm_ps = psum.tile([P, P], F32, name="warm_ps", tag="e_ps", bufs=2)
+        for i in range(WARM_PASSES):
+            nc.tensor.matmul_mx(
+                out=warm_ps[:],
+                lhsT=zero_w[:].bitcast(FP8X4),
+                lhsT_scale=zero_sc[:],
+                rhs=zero_w[:].bitcast(FP8X4),
+                rhs_scale=zero_sc[:],
+                start=True,
+                stop=True,
+            )
+
+        permute_conn(0, 0, 2)
+        permute_conn(0, 2, 4)
+        nc.vector.memset(gain_sq[:], 0.0)
+        permute_conn(1, 0, 4)
+        nc.vector.tensor_copy(out=gain_sq[:PACK, :], in_=gain_rows[:])
+        nc.vector.memset(rate_sc[1][:].rearrange("p k c -> p (k c)").bitcast(I32), 0)
+
+        load_rate_words(1, nc.sync)
+        load_lead(0)
+        load_lead(1)
+        load_rate_scales(1)
+        load_rate_words(2, nc.sync)
+        load_bg(0)
+        nc.sync.dma_start(out=calib_all[:], in_=calib.partition_broadcast(P))
+        load_rate_words(3, nc.sync)
+        load_bg(1)
+        load_bg(2)
+
+        chunk_t0 = starts(CHUNKS)
+        last = len(CHUNKS) - 1
+        u_ps = {}
+        sig = {}
+        p_bf = {}
+        p_w = {}
+        p_sc = {}
+        e_ps = {}
+        tsum = {}
+        y = {}
+        y_bf = {}
+        yt_ps = {}
+        yt = {}
+
+        def spread_gain():
+            for g in range(FG):
+                nc.tensor.transpose(gain_ps[:, g, :], gain_sq[:, P * g : P * (g + 1)], ident[:])
+
+        def stage1(c, g, u):
+            n = CHUNKS[c]
+            per_bank = BANK // n
+            if u * per_bank >= PACK:
+                return
+            i, off = locate(RATE_LOADS, chunk_t0[c])
+            j, soff = locate(RATE_SCALE_LOADS, chunk_t0[c])
+            u_ps[c, g, u] = psum.tile([P, per_bank, n], F32, name="u_ps", tag="u_ps", bufs=4)
+            for e in range(per_bank):
+                t = u * per_bank + e
+                for k in range(KP):
+                    nc.tensor.matmul_mx(
+                        out=u_ps[c, g, u][:, e, :],
+                        lhsT=conn_w[g][:, t, k, :].bitcast(FP4X4),
+                        lhsT_scale=conn_sc[g][:, t, k, :],
+                        rhs=rate_w[i][:, k, 2 * off : 2 * (off + n)].bitcast(FP4X4),
+                        rhs_scale=rate_sc[j][:, k, soff : soff + n],
+                        start=(k == 0),
+                        stop=(k == KP - 1),
+                    )
+
+        def sigmoid(c, g, u):
+            n = CHUNKS[c]
+            per_bank = BANK // n
+            if u * per_bank >= PACK:
+                return
+            if (c, g) not in sig:
+                sig[c, g] = work.tile([P, PACK // per_bank, n, per_bank], F32, name="sig", tag="sig", bufs=5, align_bytes=64)
+            nc.scalar.activation(out=sig[c, g][:, u], in_=u_ps[c, g, u][:].rearrange("p e n -> p n e"), func=ACT.Sigmoid)
+
+        def scale_p(c, g):
+            n = CHUNKS[c]
+            per_bank = BANK // n
+            p_bf[c, g] = work.tile([P, n, PACK // per_bank, per_bank], BF16, name="p_bf", tag="p_bf", bufs=3, align_bytes=64)
+            gains = gain_ps[:, g, :PACK].rearrange("p (u e) -> p u e", e=per_bank)
+            nc.vector.tensor_tensor(
+                out=p_bf[c, g][:],
+                in0=sig[c, g][:].rearrange("p u n e -> p n u e"),
+                in1=gains.unsqueeze(1).to_broadcast([P, n, PACK // per_bank, per_bank]),
+                op=ALU.mult,
+            )
+
+        def quantize_p(c, g):
+            n = CHUNKS[c]
+            p_w[c, g] = work.tile([P, PACK * n], U8, name="p_w", tag="p_w", bufs=8, align_bytes=64)
+            p_sc[c, g] = work.tile([P, n], U8, name="p_sc", tag="p_sc", bufs=8, align_bytes=64)
+            nc.vector.quantize_mx(
+                out=p_w[c, g][:].bitcast(FP8X4), scales=p_sc[c, g][:], in_=p_bf[c, g][:].rearrange("p n u e -> p (n u e)")
+            )
+
+        def stage2(c, a):
+            if a >= CHUNKS[c] // P:
+                return
+            e_ps[c, a] = psum.tile([P, S], F32, name="e_ps", tag="e_ps", bufs=2)
+            for g in range(FG):
+                nc.tensor.matmul_mx(
+                    out=e_ps[c, a][:],
+                    lhsT=p_w[c, g][:, PACK * P * a : PACK * P * (a + 1)].bitcast(FP8X4),
+                    lhsT_scale=p_sc[c, g][:, P * a : P * (a + 1)],
+                    rhs=lead_w[g][:].bitcast(FP8X4),
+                    rhs_scale=lead_sc[g][:],
+                    start=(g == 0),
+                    stop=(g == FG - 1),
+                )
+
+        def add_bg(c, a):
+            if a >= CHUNKS[c] // P:
+                return
+            i, off = locate(BG_LOADS, chunk_t0[c] + P * a)
+            tsum[c, a] = work.tile([P, S], F32, name="tsum", tag="tsum", bufs=4)
+            nc.vector.tensor_tensor(out=tsum[c, a][:], in0=e_ps[c, a][:], in1=bg[i][:, off // P, :], op=ALU.add)
+
+        def calibrate(c, a):
+            if a >= CHUNKS[c] // P:
+                return
+            if c == last:
+                round_y(c, a)
+            y[c, a] = work.tile([P, S], F32, name="y", tag="y", bufs=8)
+            engine = nc.vector if c == last else nc.gpsimd
+            engine.tensor_tensor(out=y[c, a][:], in0=tsum[c, a][:], in1=calib_all[:], op=ALU.mult)
+            t0 = chunk_t0[c] + P * a
+            nc.sync.dma_start(out=out_0[t0 : t0 + P, :], in_=y[c, a][:])
+
+        def round_y(c, a):
+            if a >= CHUNKS[c] // P or (c, a) in y_bf:
+                return
+            y_bf[c, a] = work.tile([P, 2, P, 2], BF16, name="y_bf", tag="y_bf", bufs=6)
+            order = "p (m u e) -> p u m e"
+            if c == last:
+                nc.vector.tensor_tensor(
+                    out=y_bf[c, a][:],
+                    in0=tsum[c, a][:].rearrange(order, u=2, e=2),
+                    in1=calib_all[:].rearrange(order, u=2, e=2),
+                    op=ALU.mult,
+                )
+            else:
+                nc.scalar.copy(out=y_bf[c, a][:], in_=y[c, a][:].rearrange(order, u=2, e=2))
+
+        def turn_y(c):
+            tiles = CHUNKS[c] // P
+            yt_ps[c] = psum.tile([P, tiles, 2, P], F32, name="yt_ps", tag="turn", bufs=1)
+            for a in range(tiles):
+                words = y_bf[c, a][:].rearrange("p u m e -> p (u m e)").bitcast(F32)
+                for u in range(2):
+                    nc.tensor.transpose(yt_ps[c][:, a, u, :], words[:, P * u : P * (u + 1)], ident[:])
+
+        def copy_turned(c):
+            n = CHUNKS[c]
+            yt[c] = work.tile([P, PACK * n], BF16, name="yt", tag="yt", bufs=3, align_bytes=64)
+            nc.scalar.copy(
+                out=yt[c][:].bitcast(F32).rearrange("p (a m u) -> p a m u", m=P, u=2),
+                in_=yt_ps[c][:].rearrange("p a u m -> p a m u"),
+            )
+
+        def quantize_y(c):
+            t0, t1 = chunk_t0[c], chunk_t0[c] + CHUNKS[c]
+            nc.vector.quantize_mx(out=y_w[:, PACK * t0 : PACK * t1].bitcast(FP8X4), scales=y_sc[:, t0:t1], in_=yt[c][:])
+            if t1 in CODE_STORES:
+                s0 = ([0] + CODE_STORES)[CODE_STORES.index(t1)]
+                nc.sync.dma_start(
+                    out=out_1[0].rearrange("p m t -> p (m t)").bitcast(I32)[:, s0:t1],
+                    in_=y_w[:, PACK * s0 : PACK * t1].bitcast(I32),
+                )
+            if t1 in SCALE_STORES:
+                s0 = ([0] + SCALE_STORES)[SCALE_STORES.index(t1)]
+                for q in range(4):
+                    queue = nc.scalar if t1 == T and q % 2 else nc.sync
+                    queue.dma_start(
+                        out=out_2[0, 4 * q : 4 * q + 4, s0:t1].bitcast(I32),
+                        in_=y_sc[32 * q : 32 * q + 4, s0:t1].bitcast(I32),
+                    )
+
+        period = [
+            (turn_y, 5, ()),
+            (round_y, 4, (0,)),
+            (quantize_p, 2, (1,)),
+            (stage1, 1, (1, 1,)),
+            (scale_p, 1, (0,)),
+            (add_bg, 3, (1,)),
+            (stage1, 0, (0, 0,)),
+            (sigmoid, 1, (1, 0,)),
+            (sigmoid, 1, (1, 1,)),
+            (quantize_p, 1, (0,)),
+            (stage2, 2, (0,)),
+            (stage1, 0, (0, 1,)),
+            (sigmoid, 0, (0, 0,)),
+            (scale_p, 1, (1,)),
+            (add_bg, 2, (0,)),
+            (stage1, 0, (1, 0,)),
+            (quantize_y, 6, ()),
+            (calibrate, 3, (1,)),
+            (calibrate, 2, (0,)),
+            (stage2, 2, (1,)),
+            (round_y, 4, (1,)),
+            (copy_turned, 5, ()),
+            (sigmoid, 0, (0, 1,)),
+        ]
+        once = [
+            (spread_gain, (), 0, 15),
+            (interleave_lead, (0,), 0, 8),
+            (quantize_lead, (0,), 2, 1),
+            (interleave_lead, (1,), 1, 5),
+            (quantize_lead, (1,), 1, 13),
+        ]
+        for i in range(last + 1 + max(lag for step, lag, args in period)):
+            for place, (step, lag, args) in enumerate(period):
+                for extra, extra_args, extra_i, extra_place in once:
+                    if (extra_i, extra_place) == (i, place):
+                        extra(*extra_args)
+                if 0 <= i - lag <= last:
+                    step(i - lag, *args)

@@ -65,9 +65,9 @@ def tile_neural_mass_eeg_k5_kernel(
         lead_sc = [kept("lead_sc%d" % g, [P, S], U8) for g in range(FG)]
         bg = [kept("bg%d" % i, [P, w // P, S], BF16) for i, w in enumerate(BG_LOADS)]
         calib_all = kept("calib_all", [P, S], BF16)
-        gain_rows = kept("gain_rows", [PACK, FG * P], BF16)
-        gain_sq = kept("gain_sq", [P, FG * P], F32)
-        gain_ps = psum.tile([P, FG, P], F32, name="gain_ps", tag="gain_ps", bufs=1)
+        gain_rows = kept("gain_rows", [FG, K_PASS], BF16)
+        gain_sq = kept("gain_sq", [P, PACK, P], F32)
+        gain_ps = psum.tile([P, PACK, P], F32, name="gain_ps", tag="gain_ps", bufs=1)
         zero_bf = kept("zero_bf", [P, K_PASS], BF16)
         zero_w = kept("zero_w", [P, K_PASS], U8)
         zero_sc = kept("zero_sc", [P, P], U8)
@@ -82,22 +82,22 @@ def tile_neural_mass_eeg_k5_kernel(
         conn_scales32 = conn_scales.bitcast(I32)
 
         def load_conn_words(g):
-            nc.gpsimd.dma_start(
+            nc.sync.dma_start(
                 out=conn_raw[g][:].bitcast(I32),
                 in_=conn_words32[:, :, 256 * g : 256 * (g + 1)].rearrange("k p c -> p k c"),
             )
 
-        def load_rate_words(i, queue):
+        def load_rate_words(i):
             t0 = starts(RATE_LOADS)[i]
-            queue.dma_start(
+            nc.sync.dma_start(
                 out=rate_w[i][:].bitcast(I32),
                 in_=rate_words32[:, :, t0 // 2 : (t0 + RATE_LOADS[i]) // 2].rearrange("k p c -> p k c"),
             )
 
-        def load_rate_scales(i):
+        def load_rate_scales(i, queues):
             t0 = starts(RATE_SCALE_LOADS)[i]
             for q in range(4):
-                nc.sync.dma_start(
+                queues[q].dma_start(
                     out=rate_sc[i][32 * q : 32 * q + 4].bitcast(I32),
                     in_=rate_scales32[:, 4 * q : 4 * q + 4, t0 // 4 : (t0 + RATE_SCALE_LOADS[i]) // 4].rearrange(
                         "k r c -> r k c"
@@ -117,10 +117,7 @@ def tile_neural_mass_eeg_k5_kernel(
                 nc.sync.dma_start(out=lead_raw[g][r:P:4], in_=rows[r])
 
         def load_gain():
-            nc.gpsimd.dma_start(
-                out=gain_rows[:].rearrange("t (q r) -> t q r", r=4),
-                in_=gain.rearrange("(q t r) -> t q r", t=PACK, r=4),
-            )
+            nc.sync.dma_start(out=gain_rows[:], in_=gain.rearrange("(g f) -> g f", g=FG))
 
         def load_bg(i):
             t0 = starts(BG_LOADS)[i]
@@ -148,19 +145,19 @@ def tile_neural_mass_eeg_k5_kernel(
                 out=lead_w[g][:].bitcast(FP8X4), scales=lead_sc[g][:], in_=lead_il[g][:].rearrange("p s t -> p (s t)")
             )
 
+        nc.gpsimd.memset(rate_sc[0][:].rearrange("p k c -> p (k c)").bitcast(I32), 0)
+        nc.vector.memset(conn_sc_raw[:].rearrange("p k c -> p (k c)").bitcast(I32), 0)
         load_conn_words(0)
-        load_rate_words(0, nc.gpsimd)
+        load_rate_words(0)
+        load_rate_scales(0, [nc.gpsimd, nc.gpsimd, nc.sync, nc.sync])
+        load_conn_scales()
         load_conn_words(1)
         load_gain()
         make_identity(nc, ident[:])
 
-        nc.vector.memset(conn_sc_raw[:].rearrange("p k c -> p (k c)").bitcast(I32), 0)
-        nc.vector.memset(rate_sc[0][:].rearrange("p k c -> p (k c)").bitcast(I32), 0)
         nc.vector.memset(zero_bf[:], 0.0)
         nc.vector.memset(warm[:], 0.0)
         nc.vector.quantize_mx(out=zero_w[:].bitcast(FP8X4), scales=zero_sc[:], in_=zero_bf[:])
-        load_rate_scales(0)
-        load_conn_scales()
         nc.scalar.activation(out=warm[:], in_=warm[:], func=ACT.Sigmoid)
         warm_ps = psum.tile([P, P], F32, name="warm_ps", tag="e_ps", bufs=2)
         for i in range(WARM_PASSES):
@@ -177,18 +174,22 @@ def tile_neural_mass_eeg_k5_kernel(
         permute_conn(0, 0, 2)
         permute_conn(0, 2, 4)
         nc.vector.memset(gain_sq[:], 0.0)
-        permute_conn(1, 0, 4)
-        nc.vector.tensor_copy(out=gain_sq[:PACK, :], in_=gain_rows[:])
         nc.vector.memset(rate_sc[1][:].rearrange("p k c -> p (k c)").bitcast(I32), 0)
+        permute_conn(1, 0, 2)
+        permute_conn(1, 2, 4)
+        nc.vector.tensor_copy(
+            out=gain_sq[:FG].rearrange("g t (q r) -> g t q r", r=4),
+            in_=gain_rows[:].rearrange("g (q t r) -> g t q r", t=PACK, r=4),
+        )
 
-        load_rate_words(1, nc.sync)
+        load_rate_words(1)
         load_lead(0)
         load_lead(1)
-        load_rate_scales(1)
-        load_rate_words(2, nc.sync)
+        load_rate_scales(1, [nc.sync] * 4)
+        load_rate_words(2)
         load_bg(0)
         nc.sync.dma_start(out=calib_all[:], in_=calib.partition_broadcast(P))
-        load_rate_words(3, nc.sync)
+        load_rate_words(3)
         load_bg(1)
         load_bg(2)
 
@@ -207,8 +208,8 @@ def tile_neural_mass_eeg_k5_kernel(
         yt = {}
 
         def spread_gain():
-            for g in range(FG):
-                nc.tensor.transpose(gain_ps[:, g, :], gain_sq[:, P * g : P * (g + 1)], ident[:])
+            for t in range(PACK):
+                nc.tensor.transpose(gain_ps[:, t, :], gain_sq[:, t, :], ident[:])
 
         def stage1(c, g, u):
             n = CHUNKS[c]
@@ -244,7 +245,7 @@ def tile_neural_mass_eeg_k5_kernel(
             n = CHUNKS[c]
             per_bank = BANK // n
             p_bf[c, g] = work.tile([P, n, PACK // per_bank, per_bank], BF16, name="p_bf", tag="p_bf", bufs=3, align_bytes=64)
-            gains = gain_ps[:, g, :PACK].rearrange("p (u e) -> p u e", e=per_bank)
+            gains = gain_ps[:, :, g].rearrange("p (u e) -> p u e", e=per_bank)
             nc.vector.tensor_tensor(
                 out=p_bf[c, g][:],
                 in0=sig[c, g][:].rearrange("p u n e -> p n u e"),
@@ -368,8 +369,8 @@ def tile_neural_mass_eeg_k5_kernel(
             (sigmoid, 0, (0, 1,)),
         ]
         once = [
-            (spread_gain, (), 0, 15),
-            (interleave_lead, (0,), 0, 8),
+            (spread_gain, (), 0, 16),
+            (interleave_lead, (0,), 0, 16),
             (quantize_lead, (0,), 2, 1),
             (interleave_lead, (1,), 1, 5),
             (quantize_lead, (1,), 1, 13),

@@ -25,8 +25,8 @@ CHUNKS = [256] * 7 + [128] * 2
 RATE_LOADS = [256, 256, 512, 1024]
 RATE_SCALE_LOADS = [512, 1536]
 BG_LOADS = [512, 512, 1024]
-CODE_STORES = [512, 1024, 1536, 1792, 1920, 2048]
-SCALE_STORES = [1792, 2048]
+CODE_STORES = [512, 1024, 1536, 1920, 2048]
+SCALE_STORES = [1024, 2048]
 WARM_PASSES = 20
 
 
@@ -218,7 +218,7 @@ def tile_neural_mass_eeg_k5_kernel(
                 return
             i, off = locate(RATE_LOADS, chunk_t0[c])
             j, soff = locate(RATE_SCALE_LOADS, chunk_t0[c])
-            u_ps[c, g, u] = psum.tile([P, per_bank, n], F32, name="u_ps", tag="u_ps", bufs=4)
+            u_ps[c, g, u] = psum.tile([P, per_bank, n], F32, name="u_ps", tag="u_ps", bufs=3)
             for e in range(per_bank):
                 t = u * per_bank + e
                 for k in range(KP):
@@ -244,21 +244,24 @@ def tile_neural_mass_eeg_k5_kernel(
         def scale_p(c, g):
             n = CHUNKS[c]
             per_bank = BANK // n
-            p_bf[c, g] = work.tile([P, n, PACK // per_bank, per_bank], BF16, name="p_bf", tag="p_bf", bufs=3, align_bytes=64)
+            if c not in p_bf:
+                p_bf[c] = work.tile([P, FG, n, PACK // per_bank, per_bank], BF16, name="p_bf", tag="p_bf", bufs=3, align_bytes=64)
             gains = gain_ps[:, :, g].rearrange("p (u e) -> p u e", e=per_bank)
             nc.vector.tensor_tensor(
-                out=p_bf[c, g][:],
+                out=p_bf[c][:, g],
                 in0=sig[c, g][:].rearrange("p u n e -> p n u e"),
                 in1=gains.unsqueeze(1).to_broadcast([P, n, PACK // per_bank, per_bank]),
                 op=ALU.mult,
             )
 
-        def quantize_p(c, g):
+        def quantize_p(c):
             n = CHUNKS[c]
-            p_w[c, g] = work.tile([P, PACK * n], U8, name="p_w", tag="p_w", bufs=8, align_bytes=64)
-            p_sc[c, g] = work.tile([P, n], U8, name="p_sc", tag="p_sc", bufs=8, align_bytes=64)
+            p_w[c] = work.tile([P, FG, PACK * n], U8, name="p_w", tag="p_w", bufs=4, align_bytes=64)
+            p_sc[c] = work.tile([P, FG, n], U8, name="p_sc", tag="p_sc", bufs=4, align_bytes=64)
             nc.vector.quantize_mx(
-                out=p_w[c, g][:].bitcast(FP8X4), scales=p_sc[c, g][:], in_=p_bf[c, g][:].rearrange("p n u e -> p (n u e)")
+                out=p_w[c][:].rearrange("p g w -> p (g w)").bitcast(FP8X4),
+                scales=p_sc[c][:].rearrange("p g n -> p (g n)"),
+                in_=p_bf[c][:].rearrange("p g n u e -> p (g n u e)"),
             )
 
         def stage2(c, a):
@@ -268,8 +271,8 @@ def tile_neural_mass_eeg_k5_kernel(
             for g in range(FG):
                 nc.tensor.matmul_mx(
                     out=e_ps[c, a][:],
-                    lhsT=p_w[c, g][:, PACK * P * a : PACK * P * (a + 1)].bitcast(FP8X4),
-                    lhsT_scale=p_sc[c, g][:, P * a : P * (a + 1)],
+                    lhsT=p_w[c][:, g, PACK * P * a : PACK * P * (a + 1)].bitcast(FP8X4),
+                    lhsT_scale=p_sc[c][:, g, P * a : P * (a + 1)],
                     rhs=lead_w[g][:].bitcast(FP8X4),
                     rhs_scale=lead_sc[g][:],
                     start=(g == 0),
@@ -289,7 +292,7 @@ def tile_neural_mass_eeg_k5_kernel(
             if c == last:
                 round_y(c, a)
             y[c, a] = work.tile([P, S], F32, name="y", tag="y", bufs=8)
-            engine = nc.vector if c == last else nc.gpsimd
+            engine = nc.vector if c >= last - 1 else nc.gpsimd
             engine.tensor_tensor(out=y[c, a][:], in0=tsum[c, a][:], in1=calib_all[:], op=ALU.mult)
             t0 = chunk_t0[c] + P * a
             nc.sync.dma_start(out=out_0[t0 : t0 + P, :], in_=y[c, a][:])
@@ -297,7 +300,7 @@ def tile_neural_mass_eeg_k5_kernel(
         def round_y(c, a):
             if a >= CHUNKS[c] // P or (c, a) in y_bf:
                 return
-            y_bf[c, a] = work.tile([P, 2, P, 2], BF16, name="y_bf", tag="y_bf", bufs=6)
+            y_bf[c, a] = work.tile([P, 2, P, 2], BF16, name="y_bf", tag="y_bf", bufs=12)
             order = "p (m u e) -> p u m e"
             if c == last:
                 nc.vector.tensor_tensor(
@@ -311,7 +314,7 @@ def tile_neural_mass_eeg_k5_kernel(
 
         def turn_y(c):
             tiles = CHUNKS[c] // P
-            yt_ps[c] = psum.tile([P, tiles, 2, P], F32, name="yt_ps", tag="turn", bufs=1)
+            yt_ps[c] = psum.tile([P, tiles, 2, P], F32, name="yt_ps", tag="turn", bufs=2)
             for a in range(tiles):
                 words = y_bf[c, a][:].rearrange("p u m e -> p (u m e)").bitcast(F32)
                 for u in range(2):
@@ -344,36 +347,35 @@ def tile_neural_mass_eeg_k5_kernel(
                     )
 
         period = [
-            (turn_y, 5, ()),
-            (round_y, 4, (0,)),
-            (quantize_p, 2, (1,)),
-            (stage1, 1, (1, 1,)),
+            (stage1, 1, (1, 0,)),
+            (copy_turned, 8, ()),
+            (quantize_p, 2, ()),
             (scale_p, 1, (0,)),
-            (add_bg, 3, (1,)),
             (stage1, 0, (0, 0,)),
-            (sigmoid, 1, (1, 0,)),
+            (round_y, 4, (0,)),
             (sigmoid, 1, (1, 1,)),
-            (quantize_p, 1, (0,)),
-            (stage2, 2, (0,)),
             (stage1, 0, (0, 1,)),
-            (sigmoid, 0, (0, 0,)),
-            (scale_p, 1, (1,)),
-            (add_bg, 2, (0,)),
-            (stage1, 0, (1, 0,)),
-            (quantize_y, 6, ()),
-            (calibrate, 3, (1,)),
-            (calibrate, 2, (0,)),
-            (stage2, 2, (1,)),
+            (add_bg, 3, (1,)),
+            (turn_y, 7, ()),
+            (quantize_y, 8, ()),
+            (calibrate, 4, (1,)),
+            (calibrate, 3, (0,)),
+            (stage2, 2, (0,)),
             (round_y, 4, (1,)),
-            (copy_turned, 5, ()),
+            (sigmoid, 1, (1, 0,)),
+            (sigmoid, 0, (0, 0,)),
             (sigmoid, 0, (0, 1,)),
+            (scale_p, 1, (1,)),
+            (stage2, 2, (1,)),
+            (stage1, 0, (1, 1,)),
+            (add_bg, 2, (0,)),
         ]
         once = [
+            (interleave_lead, (0,), 0, 1),
+            (quantize_lead, (0,), 1, 21),
+            (interleave_lead, (1,), 1, 0),
+            (quantize_lead, (1,), 1, 6),
             (spread_gain, (), 0, 16),
-            (interleave_lead, (0,), 0, 16),
-            (quantize_lead, (0,), 2, 1),
-            (interleave_lead, (1,), 1, 5),
-            (quantize_lead, (1,), 1, 13),
         ]
         for i in range(last + 1 + max(lag for step, lag, args in period)):
             for place, (step, lag, args) in enumerate(period):

@@ -27,7 +27,7 @@ RATE_SCALE_LOADS = [512, 1536]
 BG_LOADS = [512, 512, 1024]
 CODE_STORES = [512, 1024, 1536, 1920, 2048]
 SCALE_STORES = [1024, 2048]
-WARM_PASSES = 20
+WARM_PASSES = (12, 6)
 
 
 def starts(widths):
@@ -117,18 +117,21 @@ def tile_neural_mass_eeg_k5_kernel(
                 nc.sync.dma_start(out=lead_raw[g][r:P:4], in_=rows[r])
 
         def load_gain():
-            nc.sync.dma_start(out=gain_rows[:], in_=gain.rearrange("(g f) -> g f", g=FG))
+            nc.scalar.dma_start(out=gain_rows[:], in_=gain.rearrange("(g f) -> g f", g=FG))
 
         def load_bg(i):
             t0 = starts(BG_LOADS)[i]
             nc.sync.dma_start(out=bg[i][:], in_=background[t0 : t0 + BG_LOADS[i], :].rearrange("(a p) s -> p a s", p=P))
 
-        def permute_conn(g, t0, t1):
+        def permute_conn_words(g, t0, t1):
             n = t1 - t0
             nc.vector.tensor_copy(
                 out=conn_w[g][:, t0:t1].rearrange("p t k c -> p (t k c)").bitcast(I32).rearrange("p (t m w) -> p t m w", t=n, w=2),
                 in_=conn_raw[g][:].rearrange("p k c -> p (k c)").bitcast(I32).rearrange("p (m t w) -> p t m w", t=PACK, w=2)[:, t0:t1],
             )
+
+        def permute_conn_scales(g, t0, t1):
+            n = t1 - t0
             nc.vector.tensor_copy(
                 out=conn_sc[g][:, t0:t1].rearrange("p t k c -> p (t k c)").bitcast(I32).rearrange("p (t k m) -> p t k m", t=n, k=KP),
                 in_=conn_sc_raw[:].bitcast(I32)[:, :, P * g : P * (g + 1)].rearrange("p k (m t) -> p t k m", t=PACK)[:, t0:t1],
@@ -147,40 +150,49 @@ def tile_neural_mass_eeg_k5_kernel(
 
         nc.gpsimd.memset(rate_sc[0][:].rearrange("p k c -> p (k c)").bitcast(I32), 0)
         nc.vector.memset(conn_sc_raw[:].rearrange("p k c -> p (k c)").bitcast(I32), 0)
+        load_gain()
         load_conn_words(0)
         load_rate_words(0)
-        load_rate_scales(0, [nc.gpsimd, nc.gpsimd, nc.sync, nc.sync])
         load_conn_scales()
+        load_rate_scales(0, [nc.gpsimd, nc.gpsimd, nc.sync, nc.sync])
         load_conn_words(1)
-        load_gain()
         make_identity(nc, ident[:])
 
         nc.vector.memset(zero_bf[:], 0.0)
         nc.vector.memset(warm[:], 0.0)
         nc.vector.quantize_mx(out=zero_w[:].bitcast(FP8X4), scales=zero_sc[:], in_=zero_bf[:])
         nc.scalar.activation(out=warm[:], in_=warm[:], func=ACT.Sigmoid)
-        warm_ps = psum.tile([P, P], F32, name="warm_ps", tag="e_ps", bufs=2)
-        for i in range(WARM_PASSES):
-            nc.tensor.matmul_mx(
-                out=warm_ps[:],
-                lhsT=zero_w[:].bitcast(FP8X4),
-                lhsT_scale=zero_sc[:],
-                rhs=zero_w[:].bitcast(FP8X4),
-                rhs_scale=zero_sc[:],
-                start=True,
-                stop=True,
-            )
-
-        permute_conn(0, 0, 2)
-        permute_conn(0, 2, 4)
         nc.vector.memset(gain_sq[:], 0.0)
-        nc.vector.memset(rate_sc[1][:].rearrange("p k c -> p (k c)").bitcast(I32), 0)
-        permute_conn(1, 0, 2)
-        permute_conn(1, 2, 4)
         nc.vector.tensor_copy(
             out=gain_sq[:FG].rearrange("g t (q r) -> g t q r", r=4),
             in_=gain_rows[:].rearrange("g (q t r) -> g t q r", t=PACK, r=4),
         )
+        warm_ps = psum.tile([P, P], F32, name="warm_ps", tag="e_ps", bufs=2)
+
+        def warm_up(passes):
+            for i in range(passes):
+                nc.tensor.matmul_mx(
+                    out=warm_ps[:],
+                    lhsT=zero_w[:].bitcast(FP8X4),
+                    lhsT_scale=zero_sc[:],
+                    rhs=zero_w[:].bitcast(FP8X4),
+                    rhs_scale=zero_sc[:],
+                    start=True,
+                    stop=True,
+                )
+
+        warm_up(WARM_PASSES[0])
+        for t in range(PACK):
+            nc.tensor.transpose(gain_ps[:, t, :], gain_sq[:, t, :], ident[:])
+        warm_up(WARM_PASSES[1])
+
+        permute_conn_words(0, 0, 4)
+        permute_conn_scales(0, 2, 4)
+        permute_conn_scales(0, 0, 2)
+        nc.vector.memset(rate_sc[1][:].rearrange("p k c -> p (k c)").bitcast(I32), 0)
+        permute_conn_scales(1, 0, 4)
+        permute_conn_words(1, 2, 4)
+        permute_conn_words(1, 0, 2)
 
         load_rate_words(1)
         load_lead(0)
@@ -206,10 +218,6 @@ def tile_neural_mass_eeg_k5_kernel(
         y_bf = {}
         yt_ps = {}
         yt = {}
-
-        def spread_gain():
-            for t in range(PACK):
-                nc.tensor.transpose(gain_ps[:, t, :], gain_sq[:, t, :], ident[:])
 
         def stage1(c, g, u):
             n = CHUNKS[c]
@@ -284,7 +292,7 @@ def tile_neural_mass_eeg_k5_kernel(
                 return
             i, off = locate(BG_LOADS, chunk_t0[c] + P * a)
             tsum[c, a] = work.tile([P, S], F32, name="tsum", tag="tsum", bufs=4)
-            nc.vector.tensor_tensor(out=tsum[c, a][:], in0=e_ps[c, a][:], in1=bg[i][:, off // P, :], op=ALU.add)
+            nc.vector.tensor_tensor(out=tsum[c, a][:], in0=bg[i][:, off // P, :], in1=e_ps[c, a][:], op=ALU.add)
 
         def calibrate(c, a):
             if a >= CHUNKS[c] // P:
@@ -347,35 +355,34 @@ def tile_neural_mass_eeg_k5_kernel(
                     )
 
         period = [
+            (stage1, 0, (0, 1,)),
+            (sigmoid, 1, (1, 1,)),
             (stage1, 1, (1, 0,)),
             (copy_turned, 8, ()),
             (quantize_p, 2, ()),
-            (scale_p, 1, (0,)),
-            (stage1, 0, (0, 0,)),
-            (round_y, 4, (0,)),
-            (sigmoid, 1, (1, 1,)),
-            (stage1, 0, (0, 1,)),
-            (add_bg, 3, (1,)),
-            (turn_y, 7, ()),
-            (quantize_y, 8, ()),
             (calibrate, 4, (1,)),
-            (calibrate, 3, (0,)),
-            (stage2, 2, (0,)),
-            (round_y, 4, (1,)),
-            (sigmoid, 1, (1, 0,)),
-            (sigmoid, 0, (0, 0,)),
+            (scale_p, 1, (0,)),
+            (add_bg, 3, (1,)),
             (sigmoid, 0, (0, 1,)),
-            (scale_p, 1, (1,)),
-            (stage2, 2, (1,)),
+            (stage1, 0, (0, 0,)),
+            (turn_y, 7, ()),
             (stage1, 0, (1, 1,)),
+            (quantize_y, 8, ()),
+            (stage2, 2, (0,)),
+            (round_y, 4, (0,)),
+            (stage2, 2, (1,)),
+            (sigmoid, 1, (1, 0,)),
+            (scale_p, 1, (1,)),
+            (sigmoid, 0, (0, 0,)),
+            (calibrate, 3, (0,)),
+            (round_y, 4, (1,)),
             (add_bg, 2, (0,)),
         ]
         once = [
-            (interleave_lead, (0,), 0, 1),
-            (quantize_lead, (0,), 1, 21),
-            (interleave_lead, (1,), 1, 0),
-            (quantize_lead, (1,), 1, 6),
-            (spread_gain, (), 0, 16),
+            (interleave_lead, (0,), 0, 0),
+            (quantize_lead, (0,), 0, 16),
+            (interleave_lead, (1,), 1, 1),
+            (quantize_lead, (1,), 1, 20),
         ]
         for i in range(last + 1 + max(lag for step, lag, args in period)):
             for place, (step, lag, args) in enumerate(period):

@@ -27,7 +27,7 @@ RATE_SCALE_LOADS = [512, 1536]
 BG_LOADS = [512, 512, 1024]
 CODE_STORES = [512, 1024, 1536, 1920, 2048]
 SCALE_STORES = [1024, 2048]
-WARM_PASSES = (12, 6)
+WARM_PASSES = (12, 4)
 
 
 def starts(widths):
@@ -65,9 +65,9 @@ def tile_neural_mass_eeg_k5_kernel(
         lead_sc = [kept("lead_sc%d" % g, [P, S], U8) for g in range(FG)]
         bg = [kept("bg%d" % i, [P, w // P, S], BF16) for i, w in enumerate(BG_LOADS)]
         calib_all = kept("calib_all", [P, S], BF16)
-        gain_rows = kept("gain_rows", [FG, K_PASS], BF16)
-        gain_sq = kept("gain_sq", [P, PACK, P], F32)
-        gain_ps = psum.tile([P, PACK, P], F32, name="gain_ps", tag="gain_ps", bufs=1)
+        gain_row = kept("gain_row", [1, F], BF16)
+        gain_sq = kept("gain_sq", [P, FG * PACK, P], F32)
+        gain_ps = psum.tile([P, BANK], F32, name="gain_ps", tag="gain_ps", bufs=1)
         zero_bf = kept("zero_bf", [P, K_PASS], BF16)
         zero_w = kept("zero_w", [P, K_PASS], U8)
         zero_sc = kept("zero_sc", [P, P], U8)
@@ -117,7 +117,7 @@ def tile_neural_mass_eeg_k5_kernel(
                 nc.sync.dma_start(out=lead_raw[g][r:P:4], in_=rows[r])
 
         def load_gain():
-            nc.scalar.dma_start(out=gain_rows[:], in_=gain.rearrange("(g f) -> g f", g=FG))
+            nc.scalar.dma_start(out=gain_row[:], in_=gain.rearrange("(o f) -> o f", o=1))
 
         def load_bg(i):
             t0 = starts(BG_LOADS)[i]
@@ -138,10 +138,20 @@ def tile_neural_mass_eeg_k5_kernel(
             )
 
         def interleave_lead(g):
-            nc.vector.tensor_copy(
-                out=lead_il[g][:].rearrange("p (c i) t -> p c t i", i=4),
-                in_=lead_raw[g][:].rearrange("p t (c i) -> p c t i", i=4),
-            )
+            if g == 0:
+                nc.vector.tensor_copy(
+                    out=lead_il[g][:].rearrange("p (c i) t -> p c t i", i=4),
+                    in_=lead_raw[g][:].rearrange("p t (c i) -> p c t i", i=4),
+                )
+            else:
+                nc.gpsimd.tensor_scalar(
+                    out=lead_il[g][:],
+                    in0=lead_raw[g][:].rearrange("p t s -> p s t"),
+                    scalar1=1.0,
+                    scalar2=0.0,
+                    op0=ALU.mult,
+                    op1=ALU.add,
+                )
 
         def quantize_lead(g):
             nc.vector.quantize_mx(
@@ -163,10 +173,11 @@ def tile_neural_mass_eeg_k5_kernel(
         nc.vector.quantize_mx(out=zero_w[:].bitcast(FP8X4), scales=zero_sc[:], in_=zero_bf[:])
         nc.scalar.activation(out=warm[:], in_=warm[:], func=ACT.Sigmoid)
         nc.vector.memset(gain_sq[:], 0.0)
-        nc.vector.tensor_copy(
-            out=gain_sq[:FG].rearrange("g t (q r) -> g t q r", r=4),
-            in_=gain_rows[:].rearrange("g (q t r) -> g t q r", t=PACK, r=4),
-        )
+        for g in range(FG):
+            nc.vector.tensor_copy(
+                out=gain_sq[:1, PACK * g : PACK * (g + 1), :].rearrange("o t (q r) -> o t q r", r=4),
+                in_=gain_row[:, K_PASS * g : K_PASS * (g + 1)].rearrange("o (q t r) -> o t q r", t=PACK, r=4),
+            )
         warm_ps = psum.tile([P, P], F32, name="warm_ps", tag="e_ps", bufs=2)
 
         def warm_up(passes):
@@ -182,8 +193,8 @@ def tile_neural_mass_eeg_k5_kernel(
                 )
 
         warm_up(WARM_PASSES[0])
-        for t in range(PACK):
-            nc.tensor.transpose(gain_ps[:, t, :], gain_sq[:, t, :], ident[:])
+        for j in range(FG * PACK):
+            nc.tensor.transpose(gain_ps[:, j : j + P], gain_sq[:, j, :], ident[:])
         warm_up(WARM_PASSES[1])
 
         permute_conn_words(0, 0, 4)
@@ -191,8 +202,8 @@ def tile_neural_mass_eeg_k5_kernel(
         permute_conn_scales(0, 0, 2)
         nc.vector.memset(rate_sc[1][:].rearrange("p k c -> p (k c)").bitcast(I32), 0)
         permute_conn_scales(1, 0, 4)
-        permute_conn_words(1, 2, 4)
         permute_conn_words(1, 0, 2)
+        permute_conn_words(1, 2, 4)
 
         load_rate_words(1)
         load_lead(0)
@@ -254,7 +265,7 @@ def tile_neural_mass_eeg_k5_kernel(
             per_bank = BANK // n
             if c not in p_bf:
                 p_bf[c] = work.tile([P, FG, n, PACK // per_bank, per_bank], BF16, name="p_bf", tag="p_bf", bufs=3, align_bytes=64)
-            gains = gain_ps[:, :, g].rearrange("p (u e) -> p u e", e=per_bank)
+            gains = gain_ps[:, PACK * g : PACK * (g + 1)].rearrange("p (u e) -> p u e", e=per_bank)
             nc.vector.tensor_tensor(
                 out=p_bf[c][:, g],
                 in0=sig[c, g][:].rearrange("p u n e -> p n u e"),
@@ -297,8 +308,6 @@ def tile_neural_mass_eeg_k5_kernel(
         def calibrate(c, a):
             if a >= CHUNKS[c] // P:
                 return
-            if c == last:
-                round_y(c, a)
             y[c, a] = work.tile([P, S], F32, name="y", tag="y", bufs=8)
             engine = nc.vector if c >= last - 1 else nc.gpsimd
             engine.tensor_tensor(out=y[c, a][:], in0=tsum[c, a][:], in1=calib_all[:], op=ALU.mult)
@@ -306,19 +315,10 @@ def tile_neural_mass_eeg_k5_kernel(
             nc.sync.dma_start(out=out_0[t0 : t0 + P, :], in_=y[c, a][:])
 
         def round_y(c, a):
-            if a >= CHUNKS[c] // P or (c, a) in y_bf:
+            if a >= CHUNKS[c] // P:
                 return
             y_bf[c, a] = work.tile([P, 2, P, 2], BF16, name="y_bf", tag="y_bf", bufs=12)
-            order = "p (m u e) -> p u m e"
-            if c == last:
-                nc.vector.tensor_tensor(
-                    out=y_bf[c, a][:],
-                    in0=tsum[c, a][:].rearrange(order, u=2, e=2),
-                    in1=calib_all[:].rearrange(order, u=2, e=2),
-                    op=ALU.mult,
-                )
-            else:
-                nc.scalar.copy(out=y_bf[c, a][:], in_=y[c, a][:].rearrange(order, u=2, e=2))
+            nc.scalar.copy(out=y_bf[c, a][:], in_=y[c, a][:].rearrange("p (m u e) -> p u m e", u=2, e=2))
 
         def turn_y(c):
             tiles = CHUNKS[c] // P
@@ -330,7 +330,7 @@ def tile_neural_mass_eeg_k5_kernel(
 
         def copy_turned(c):
             n = CHUNKS[c]
-            yt[c] = work.tile([P, PACK * n], BF16, name="yt", tag="yt", bufs=3, align_bytes=64)
+            yt[c] = work.tile([P, PACK * n], BF16, name="yt", tag="yt", bufs=4, align_bytes=64)
             nc.scalar.copy(
                 out=yt[c][:].bitcast(F32).rearrange("p (a m u) -> p a m u", m=P, u=2),
                 in_=yt_ps[c][:].rearrange("p a u m -> p a m u"),
@@ -355,34 +355,34 @@ def tile_neural_mass_eeg_k5_kernel(
                     )
 
         period = [
-            (stage1, 0, (0, 1,)),
-            (sigmoid, 1, (1, 1,)),
-            (stage1, 1, (1, 0,)),
-            (copy_turned, 8, ()),
-            (quantize_p, 2, ()),
-            (calibrate, 4, (1,)),
             (scale_p, 1, (0,)),
+            (sigmoid, 1, (1, 1,)),
+            (stage2, 3, (1,)),
+            (stage1, 0, (0, 1,)),
             (add_bg, 3, (1,)),
-            (sigmoid, 0, (0, 1,)),
+            (turn_y, 8, ()),
+            (copy_turned, 8, ()),
             (stage1, 0, (0, 0,)),
-            (turn_y, 7, ()),
+            (round_y, 5, (0,)),
+            (quantize_p, 2, ()),
+            (calibrate, 3, (1,)),
+            (stage2, 3, (0,)),
+            (stage1, 0, (1, 0,)),
             (stage1, 0, (1, 1,)),
-            (quantize_y, 8, ()),
-            (stage2, 2, (0,)),
-            (round_y, 4, (0,)),
-            (stage2, 2, (1,)),
-            (sigmoid, 1, (1, 0,)),
+            (sigmoid, 0, (0, 1,)),
             (scale_p, 1, (1,)),
-            (sigmoid, 0, (0, 0,)),
-            (calibrate, 3, (0,)),
             (round_y, 4, (1,)),
-            (add_bg, 2, (0,)),
+            (add_bg, 3, (0,)),
+            (sigmoid, 0, (0, 0,)),
+            (sigmoid, 0, (1, 0,)),
+            (quantize_y, 10, ()),
+            (calibrate, 3, (0,)),
         ]
         once = [
-            (interleave_lead, (0,), 0, 0),
-            (quantize_lead, (0,), 0, 16),
-            (interleave_lead, (1,), 1, 1),
-            (quantize_lead, (1,), 1, 20),
+            (interleave_lead, (0,), 0, 18),
+            (quantize_lead, (0,), 2, 8),
+            (interleave_lead, (1,), 1, 10),
+            (quantize_lead, (1,), 2, 3),
         ]
         for i in range(last + 1 + max(lag for step, lag, args in period)):
             for place, (step, lag, args) in enumerate(period):

@@ -21,13 +21,22 @@ K_PASS = P * PACK
 KP = K // K_PASS
 FG = F // K_PASS
 BANK = 512
+PART = 256
+TILES = T // P
 CHUNKS = [256] * 7 + [128] * 2
-RATE_LOADS = [256, 256, 512, 1024]
-RATE_SCALE_LOADS = [512, 1536]
+RATE_LOADS = [512, 512, 1024]
 BG_LOADS = [512, 512, 1024]
-CODE_STORES = [512, 1024, 1536, 1920, 2048]
-SCALE_STORES = [1024, 2048]
-WARM_PASSES = (12, 4)
+CODE_STORES = [512, 1024, 1536, 2048]
+SCALE_STORES = [2048]
+TURN_RUNS = [4, 4, 4, 2, 1, 1]
+WARM_PASSES = 8
+WARM_N = 256
+STAGE2_LAG = 3
+ROUND_LAG = 2
+TURN_LAG = 0
+QUANT_Y_LAG = 2
+FIRST_TILE_SLOT = 5
+VECTOR_TILES = (13, 14, 15)
 
 
 def starts(widths):
@@ -53,27 +62,29 @@ def tile_neural_mass_eeg_k5_kernel(
         def kept(name, shape, dtype):
             return keep.tile(shape, dtype, name=name, align_bytes=64)
 
+        rate_scale_loads = [512, T - 512]
         conn_raw = [kept("conn_raw%d" % g, [P, KP, 2 * K_PASS], U8) for g in range(FG)]
         conn_sc_raw = kept("conn_sc_raw", [P, KP, F], U8)
         conn_w = [kept("conn_w%d" % g, [P, PACK, KP, 2 * P], U8) for g in range(FG)]
         conn_sc = [kept("conn_sc%d" % g, [P, PACK, KP, P], U8) for g in range(FG)]
         rate_w = [kept("rate_w%d" % i, [P, KP, 2 * w], U8) for i, w in enumerate(RATE_LOADS)]
-        rate_sc = [kept("rate_sc%d" % i, [P, KP, w], U8) for i, w in enumerate(RATE_SCALE_LOADS)]
+        rate_sc = [kept("rate_sc%d" % i, [P, KP, w], U8) for i, w in enumerate(rate_scale_loads)]
         lead_raw = [kept("lead_raw%d" % g, [P, PACK, S], BF16) for g in range(FG)]
         lead_il = [kept("lead_il%d" % g, [P, S, PACK], BF16) for g in range(FG)]
         lead_w = [kept("lead_w%d" % g, [P, PACK * S], U8) for g in range(FG)]
         lead_sc = [kept("lead_sc%d" % g, [P, S], U8) for g in range(FG)]
         bg = [kept("bg%d" % i, [P, w // P, S], BF16) for i, w in enumerate(BG_LOADS)]
         calib_all = kept("calib_all", [P, S], BF16)
-        gain_row = kept("gain_row", [1, F], BF16)
-        gain_sq = kept("gain_sq", [P, FG * PACK, P], F32)
-        gain_ps = psum.tile([P, BANK], F32, name="gain_ps", tag="gain_ps", bufs=1)
-        zero_bf = kept("zero_bf", [P, K_PASS], BF16)
-        zero_w = kept("zero_w", [P, K_PASS], U8)
-        zero_sc = kept("zero_sc", [P, P], U8)
+        gain_rows = kept("gain_rows", [P, FG * P], BF16)
+        gain_ps = psum.tile([P, FG, P], BF16, name="gain_ps", tag="gain_ps", bufs=1)
+        zero_bf = kept("zero_bf", [P, PACK * WARM_N], BF16)
+        zero_w = kept("zero_w", [P, PACK * WARM_N], U8)
+        zero_sc = kept("zero_sc", [P, WARM_N], U8)
         ident = kept("ident", [P, P], F32)
+        ident_bf = kept("ident_bf", [P, P], BF16)
         warm = kept("warm", [P, 1], F32)
         y_w = kept("y_w", [P, PACK * T], U8)
+        yt = kept("yt", [P, PACK * T], BF16)
         y_sc = kept("y_sc", [P, T], U8)
 
         rate_words32 = rate_words.bitcast(I32)
@@ -81,35 +92,36 @@ def tile_neural_mass_eeg_k5_kernel(
         rate_scales32 = rate_scales.bitcast(I32)
         conn_scales32 = conn_scales.bitcast(I32)
 
+        def zero(tile):
+            nc.vector.memset(tile[:].rearrange("p k c -> p (k c)").bitcast(I32), 0)
+
         def load_conn_words(g):
             nc.sync.dma_start(
                 out=conn_raw[g][:].bitcast(I32),
                 in_=conn_words32[:, :, 256 * g : 256 * (g + 1)].rearrange("k p c -> p k c"),
             )
 
-        def load_rate_words(i):
-            t0 = starts(RATE_LOADS)[i]
+        def load_rate_words(c):
+            t0 = starts(RATE_LOADS)[c]
             nc.sync.dma_start(
-                out=rate_w[i][:].bitcast(I32),
-                in_=rate_words32[:, :, t0 // 2 : (t0 + RATE_LOADS[i]) // 2].rearrange("k p c -> p k c"),
+                out=rate_w[c][:].bitcast(I32),
+                in_=rate_words32[:, :, t0 // 2 : (t0 + RATE_LOADS[c]) // 2].rearrange("k p c -> p k c"),
             )
 
-        def load_rate_scales(i, queues):
-            t0 = starts(RATE_SCALE_LOADS)[i]
-            for q in range(4):
-                queues[q].dma_start(
-                    out=rate_sc[i][32 * q : 32 * q + 4].bitcast(I32),
-                    in_=rate_scales32[:, 4 * q : 4 * q + 4, t0 // 4 : (t0 + RATE_SCALE_LOADS[i]) // 4].rearrange(
-                        "k r c -> r k c"
-                    ),
-                )
+        def load_rate_scales(i, q, queue):
+            t0 = starts(rate_scale_loads)[i]
+            queue.dma_start(
+                out=rate_sc[i][32 * q : 32 * q + 4].bitcast(I32),
+                in_=rate_scales32[:, 4 * q : 4 * q + 4, t0 // 4 : (t0 + rate_scale_loads[i]) // 4].rearrange(
+                    "k r c -> r k c"
+                ),
+            )
 
-        def load_conn_scales():
-            for q in range(4):
-                nc.scalar.dma_start(
-                    out=conn_sc_raw[32 * q : 32 * q + 4].bitcast(I32),
-                    in_=conn_scales32[:, 4 * q : 4 * q + 4, :].rearrange("k r c -> r k c"),
-                )
+        def load_conn_scales(q, queue):
+            queue.dma_start(
+                out=conn_sc_raw[32 * q : 32 * q + 4].bitcast(I32),
+                in_=conn_scales32[:, 4 * q : 4 * q + 4, :].rearrange("k r c -> r k c"),
+            )
 
         def load_lead(g):
             rows = lead[K_PASS * g : K_PASS * (g + 1), :].rearrange("(q t r) s -> r q t s", t=PACK, r=4)
@@ -117,7 +129,10 @@ def tile_neural_mass_eeg_k5_kernel(
                 nc.sync.dma_start(out=lead_raw[g][r:P:4], in_=rows[r])
 
         def load_gain():
-            nc.scalar.dma_start(out=gain_row[:], in_=gain.rearrange("(o f) -> o f", o=1))
+            nc.sync.dma_start(
+                out=gain_rows[:PACK].rearrange("t (m r) -> t m r", r=4),
+                in_=gain.rearrange("(m t r) -> t m r", t=PACK, r=4),
+            )
 
         def load_bg(i):
             t0 = starts(BG_LOADS)[i]
@@ -137,20 +152,21 @@ def tile_neural_mass_eeg_k5_kernel(
                 in_=conn_sc_raw[:].bitcast(I32)[:, :, P * g : P * (g + 1)].rearrange("p k (m t) -> p t k m", t=PACK)[:, t0:t1],
             )
 
-        def interleave_lead(g):
-            if g == 0:
-                nc.vector.tensor_copy(
-                    out=lead_il[g][:].rearrange("p (c i) t -> p c t i", i=4),
-                    in_=lead_raw[g][:].rearrange("p t (c i) -> p c t i", i=4),
-                )
-            else:
+        def interleave_lead(g, engine, s0, s1):
+            if engine == "gpsimd":
                 nc.gpsimd.tensor_scalar(
-                    out=lead_il[g][:],
-                    in0=lead_raw[g][:].rearrange("p t s -> p s t"),
+                    out=lead_il[g][:, s0:s1, :],
+                    in0=lead_raw[g][:, :, s0:s1].rearrange("p t s -> p s t"),
                     scalar1=1.0,
                     scalar2=0.0,
                     op0=ALU.mult,
                     op1=ALU.add,
+                )
+            else:
+                copy = nc.vector.tensor_copy if engine == "vector" else nc.scalar.copy
+                copy(
+                    out=lead_il[g][:, s0:s1, :].rearrange("p (c i) t -> p c t i", i=4),
+                    in_=lead_raw[g][:, :, s0:s1].rearrange("p t (c i) -> p c t i", i=4),
                 )
 
         def quantize_lead(g):
@@ -158,67 +174,65 @@ def tile_neural_mass_eeg_k5_kernel(
                 out=lead_w[g][:].bitcast(FP8X4), scales=lead_sc[g][:], in_=lead_il[g][:].rearrange("p s t -> p (s t)")
             )
 
-        nc.gpsimd.memset(rate_sc[0][:].rearrange("p k c -> p (k c)").bitcast(I32), 0)
-        nc.vector.memset(conn_sc_raw[:].rearrange("p k c -> p (k c)").bitcast(I32), 0)
-        load_gain()
-        load_conn_words(0)
+        def turn_gain():
+            for g in range(FG):
+                nc.tensor.transpose(gain_ps[:, g, :], gain_rows[:, P * g : P * (g + 1)], ident_bf[:])
+
         load_rate_words(0)
-        load_conn_scales()
-        load_rate_scales(0, [nc.gpsimd, nc.gpsimd, nc.sync, nc.sync])
+        load_conn_words(0)
+        zero(conn_sc_raw)
+        zero(rate_sc[0])
+        load_conn_scales(0, nc.scalar)
+        load_conn_scales(1, nc.sync)
+        load_conn_scales(2, nc.scalar)
+        load_conn_scales(3, nc.sync)
+        load_rate_scales(0, 0, nc.gpsimd)
+        load_rate_scales(0, 1, nc.scalar)
+        load_rate_scales(0, 2, nc.sync)
+        load_rate_scales(0, 3, nc.sync)
         load_conn_words(1)
-        make_identity(nc, ident[:])
 
         nc.vector.memset(zero_bf[:], 0.0)
         nc.vector.memset(warm[:], 0.0)
+        nc.vector.memset(gain_rows[:], 0.0)
         nc.vector.quantize_mx(out=zero_w[:].bitcast(FP8X4), scales=zero_sc[:], in_=zero_bf[:])
         nc.scalar.activation(out=warm[:], in_=warm[:], func=ACT.Sigmoid)
-        nc.vector.memset(gain_sq[:], 0.0)
-        for g in range(FG):
-            nc.vector.tensor_copy(
-                out=gain_sq[:1, PACK * g : PACK * (g + 1), :].rearrange("o t (q r) -> o t q r", r=4),
-                in_=gain_row[:, K_PASS * g : K_PASS * (g + 1)].rearrange("o (q t r) -> o t q r", t=PACK, r=4),
+        load_gain()
+        make_identity(nc, ident_bf[:])
+        warm_ps = psum.tile([P, WARM_N], F32, name="warm_ps", tag="e_ps", bufs=2)
+        for i in range(WARM_PASSES):
+            nc.tensor.matmul_mx(
+                out=warm_ps[:],
+                lhsT=zero_w[:, : PACK * P].bitcast(FP8X4),
+                lhsT_scale=zero_sc[:, :P],
+                rhs=zero_w[:].bitcast(FP8X4),
+                rhs_scale=zero_sc[:],
+                start=True,
+                stop=True,
             )
-        warm_ps = psum.tile([P, P], F32, name="warm_ps", tag="e_ps", bufs=2)
 
-        def warm_up(passes):
-            for i in range(passes):
-                nc.tensor.matmul_mx(
-                    out=warm_ps[:],
-                    lhsT=zero_w[:].bitcast(FP8X4),
-                    lhsT_scale=zero_sc[:],
-                    rhs=zero_w[:].bitcast(FP8X4),
-                    rhs_scale=zero_sc[:],
-                    start=True,
-                    stop=True,
-                )
-
-        warm_up(WARM_PASSES[0])
-        for j in range(FG * PACK):
-            nc.tensor.transpose(gain_ps[:, j : j + P], gain_sq[:, j, :], ident[:])
-        warm_up(WARM_PASSES[1])
-
-        permute_conn_words(0, 0, 4)
-        permute_conn_scales(0, 2, 4)
+        permute_conn_words(0, 0, 2)
+        permute_conn_words(0, 2, 4)
         permute_conn_scales(0, 0, 2)
-        nc.vector.memset(rate_sc[1][:].rearrange("p k c -> p (k c)").bitcast(I32), 0)
+        permute_conn_scales(0, 2, 4)
+        zero(rate_sc[1])
+        make_identity(nc, ident[:])
         permute_conn_scales(1, 0, 4)
         permute_conn_words(1, 0, 2)
         permute_conn_words(1, 2, 4)
 
-        load_rate_words(1)
         load_lead(0)
         load_lead(1)
-        load_rate_scales(1, [nc.sync] * 4)
-        load_rate_words(2)
+        load_rate_words(1)
+        for q in range(4):
+            load_rate_scales(1, q, nc.sync)
         load_bg(0)
         nc.sync.dma_start(out=calib_all[:], in_=calib.partition_broadcast(P))
-        load_rate_words(3)
+        load_rate_words(2)
         load_bg(1)
         load_bg(2)
 
         chunk_t0 = starts(CHUNKS)
-        last = len(CHUNKS) - 1
-        u_ps = {}
         sig = {}
         p_bf = {}
         p_w = {}
@@ -228,21 +242,18 @@ def tile_neural_mass_eeg_k5_kernel(
         y = {}
         y_bf = {}
         yt_ps = {}
-        yt = {}
 
         def stage1(c, g, u):
             n = CHUNKS[c]
             per_bank = BANK // n
-            if u * per_bank >= PACK:
-                return
             i, off = locate(RATE_LOADS, chunk_t0[c])
-            j, soff = locate(RATE_SCALE_LOADS, chunk_t0[c])
-            u_ps[c, g, u] = psum.tile([P, per_bank, n], F32, name="u_ps", tag="u_ps", bufs=3)
+            j, soff = locate(rate_scale_loads, chunk_t0[c])
+            u_ps = psum.tile([P, per_bank, n], F32, name="u_ps", tag="u_ps", bufs=3)
             for e in range(per_bank):
                 t = u * per_bank + e
                 for k in range(KP):
                     nc.tensor.matmul_mx(
-                        out=u_ps[c, g, u][:, e, :],
+                        out=u_ps[:, e, :],
                         lhsT=conn_w[g][:, t, k, :].bitcast(FP4X4),
                         lhsT_scale=conn_sc[g][:, t, k, :],
                         rhs=rate_w[i][:, k, 2 * off : 2 * (off + n)].bitcast(FP4X4),
@@ -250,95 +261,95 @@ def tile_neural_mass_eeg_k5_kernel(
                         start=(k == 0),
                         stop=(k == KP - 1),
                     )
+            if u == 0:
+                sig[c, g] = work.tile([P, PACK // per_bank, n, per_bank], F32, name="sig", tag="sig", bufs=4, align_bytes=64)
+            nc.scalar.activation(out=sig[c, g][:, u], in_=u_ps[:].rearrange("p e n -> p n e"), func=ACT.Sigmoid)
 
-        def sigmoid(c, g, u):
+        def scale_p(c, g, h):
             n = CHUNKS[c]
+            w = min(n, PART)
             per_bank = BANK // n
-            if u * per_bank >= PACK:
-                return
-            if (c, g) not in sig:
-                sig[c, g] = work.tile([P, PACK // per_bank, n, per_bank], F32, name="sig", tag="sig", bufs=5, align_bytes=64)
-            nc.scalar.activation(out=sig[c, g][:, u], in_=u_ps[c, g, u][:].rearrange("p e n -> p n e"), func=ACT.Sigmoid)
+            if g == 0:
+                p_bf[c, h] = work.tile([P, FG, w, PACK], BF16, name="p_bf", tag="p_bf", bufs=3, align_bytes=64)
+            gains = gain_ps[:, g, :PACK]
+            if per_bank == 1:
+                nc.vector.tensor_tensor(
+                    out=p_bf[c, h][:, g].rearrange("p (m i) t -> p m t i", i=4),
+                    in0=sig[c, g][:, :, w * h : w * (h + 1), 0].rearrange("p t (m i) -> p m t i", i=4),
+                    in1=gains.unsqueeze(1).unsqueeze(3).to_broadcast([P, w // 4, PACK, 4]),
+                    op=ALU.mult,
+                )
+            else:
+                nc.vector.tensor_tensor(
+                    out=p_bf[c, h][:, g].rearrange("p n (u e) -> p n u e", e=per_bank),
+                    in0=sig[c, g][:].rearrange("p u n e -> p n u e"),
+                    in1=gains.rearrange("p (u e) -> p u e", e=per_bank).unsqueeze(1).to_broadcast([P, w, PACK // per_bank, per_bank]),
+                    op=ALU.mult,
+                )
 
-        def scale_p(c, g):
-            n = CHUNKS[c]
-            per_bank = BANK // n
-            if c not in p_bf:
-                p_bf[c] = work.tile([P, FG, n, PACK // per_bank, per_bank], BF16, name="p_bf", tag="p_bf", bufs=3, align_bytes=64)
-            gains = gain_ps[:, PACK * g : PACK * (g + 1)].rearrange("p (u e) -> p u e", e=per_bank)
-            nc.vector.tensor_tensor(
-                out=p_bf[c][:, g],
-                in0=sig[c, g][:].rearrange("p u n e -> p n u e"),
-                in1=gains.unsqueeze(1).to_broadcast([P, n, PACK // per_bank, per_bank]),
-                op=ALU.mult,
-            )
-
-        def quantize_p(c):
-            n = CHUNKS[c]
-            p_w[c] = work.tile([P, FG, PACK * n], U8, name="p_w", tag="p_w", bufs=4, align_bytes=64)
-            p_sc[c] = work.tile([P, FG, n], U8, name="p_sc", tag="p_sc", bufs=4, align_bytes=64)
+        def quantize_p(c, h):
+            w = min(CHUNKS[c], PART)
+            p_w[c, h] = work.tile([P, FG, PACK * w], U8, name="p_w", tag="p_w", bufs=4, align_bytes=64)
+            p_sc[c, h] = work.tile([P, FG, w], U8, name="p_sc", tag="p_sc", bufs=4, align_bytes=64)
             nc.vector.quantize_mx(
-                out=p_w[c][:].rearrange("p g w -> p (g w)").bitcast(FP8X4),
-                scales=p_sc[c][:].rearrange("p g n -> p (g n)"),
-                in_=p_bf[c][:].rearrange("p g n u e -> p (g n u e)"),
+                out=p_w[c, h][:].rearrange("p g w -> p (g w)").bitcast(FP8X4),
+                scales=p_sc[c, h][:].rearrange("p g n -> p (g n)"),
+                in_=p_bf[c, h][:].rearrange("p g n t -> p (g n t)"),
             )
 
-        def stage2(c, a):
-            if a >= CHUNKS[c] // P:
-                return
-            e_ps[c, a] = psum.tile([P, S], F32, name="e_ps", tag="e_ps", bufs=2)
+        def stage2(j):
+            c, off = locate(CHUNKS, P * j)
+            h, a = divmod(off // P, PART // P)
+            e_ps = psum.tile([P, S], F32, name="e_ps", tag="e_ps", bufs=2)
             for g in range(FG):
                 nc.tensor.matmul_mx(
-                    out=e_ps[c, a][:],
-                    lhsT=p_w[c][:, g, PACK * P * a : PACK * P * (a + 1)].bitcast(FP8X4),
-                    lhsT_scale=p_sc[c][:, g, P * a : P * (a + 1)],
+                    out=e_ps[:],
+                    lhsT=p_w[c, h][:, g, PACK * P * a : PACK * P * (a + 1)].bitcast(FP8X4),
+                    lhsT_scale=p_sc[c, h][:, g, P * a : P * (a + 1)],
                     rhs=lead_w[g][:].bitcast(FP8X4),
                     rhs_scale=lead_sc[g][:],
                     start=(g == 0),
                     stop=(g == FG - 1),
                 )
+            i, off = locate(BG_LOADS, P * j)
+            tsum[j] = work.tile([P, S], F32, name="tsum", tag="tsum", bufs=4)
+            nc.vector.tensor_tensor(out=tsum[j][:], in0=bg[i][:, off // P, :], in1=e_ps[:], op=ALU.add)
 
-        def add_bg(c, a):
-            if a >= CHUNKS[c] // P:
-                return
-            i, off = locate(BG_LOADS, chunk_t0[c] + P * a)
-            tsum[c, a] = work.tile([P, S], F32, name="tsum", tag="tsum", bufs=4)
-            nc.vector.tensor_tensor(out=tsum[c, a][:], in0=bg[i][:, off // P, :], in1=e_ps[c, a][:], op=ALU.add)
+        def calibrate(j):
+            y[j] = work.tile([P, S], F32, name="y", tag="y", bufs=6)
+            engine = nc.vector if j in VECTOR_TILES else nc.gpsimd
+            engine.tensor_tensor(out=y[j][:], in0=tsum[j][:], in1=calib_all[:], op=ALU.mult)
+            nc.sync.dma_start(out=out_0[P * j : P * (j + 1), :], in_=y[j][:])
 
-        def calibrate(c, a):
-            if a >= CHUNKS[c] // P:
-                return
-            y[c, a] = work.tile([P, S], F32, name="y", tag="y", bufs=8)
-            engine = nc.vector if c >= last - 1 else nc.gpsimd
-            engine.tensor_tensor(out=y[c, a][:], in0=tsum[c, a][:], in1=calib_all[:], op=ALU.mult)
-            t0 = chunk_t0[c] + P * a
-            nc.sync.dma_start(out=out_0[t0 : t0 + P, :], in_=y[c, a][:])
-
-        def round_y(c, a):
-            if a >= CHUNKS[c] // P:
-                return
-            y_bf[c, a] = work.tile([P, 2, P, 2], BF16, name="y_bf", tag="y_bf", bufs=12)
-            nc.scalar.copy(out=y_bf[c, a][:], in_=y[c, a][:].rearrange("p (m u e) -> p u m e", u=2, e=2))
-
-        def turn_y(c):
-            tiles = CHUNKS[c] // P
-            yt_ps[c] = psum.tile([P, tiles, 2, P], F32, name="yt_ps", tag="turn", bufs=2)
-            for a in range(tiles):
-                words = y_bf[c, a][:].rearrange("p u m e -> p (u m e)").bitcast(F32)
-                for u in range(2):
-                    nc.tensor.transpose(yt_ps[c][:, a, u, :], words[:, P * u : P * (u + 1)], ident[:])
-
-        def copy_turned(c):
-            n = CHUNKS[c]
-            yt[c] = work.tile([P, PACK * n], BF16, name="yt", tag="yt", bufs=4, align_bytes=64)
-            nc.scalar.copy(
-                out=yt[c][:].bitcast(F32).rearrange("p (a m u) -> p a m u", m=P, u=2),
-                in_=yt_ps[c][:].rearrange("p a u m -> p a m u"),
+        def round_on_vector(j):
+            y_bf[j] = work.tile([P, 2, P, 2], BF16, name="y_bf", tag="y_bf", bufs=8)
+            nc.vector.tensor_tensor(
+                out=y_bf[j][:],
+                in0=tsum[j][:].rearrange("p (m u e) -> p u m e", u=2, e=2),
+                in1=calib_all[:].rearrange("p (m u e) -> p u m e", u=2, e=2),
+                op=ALU.mult,
             )
 
-        def quantize_y(c):
-            t0, t1 = chunk_t0[c], chunk_t0[c] + CHUNKS[c]
-            nc.vector.quantize_mx(out=y_w[:, PACK * t0 : PACK * t1].bitcast(FP8X4), scales=y_sc[:, t0:t1], in_=yt[c][:])
+        def round_y(j):
+            y_bf[j] = work.tile([P, 2, P, 2], BF16, name="y_bf", tag="y_bf", bufs=8)
+            nc.scalar.copy(out=y_bf[j][:], in_=y[j][:].rearrange("p (m u e) -> p u m e", u=2, e=2))
+
+        def turn_y(j0, tiles, tag="turn", bufs=2):
+            yt_ps[j0] = psum.tile([P, tiles, 2, P], F32, name="yt_ps", tag=tag, bufs=bufs)
+            for a in range(tiles):
+                words = y_bf[j0 + a][:].rearrange("p u m e -> p (u m e)").bitcast(F32)
+                for u in range(2):
+                    nc.tensor.transpose(yt_ps[j0][:, a, u, :], words[:, P * u : P * (u + 1)], ident[:])
+
+        def copy_turned(j0, tiles, engine=nc.scalar.copy):
+            engine(
+                out=yt[:, PACK * P * j0 : PACK * P * (j0 + tiles)].bitcast(F32).rearrange("p (a m u) -> p a m u", m=P, u=2),
+                in_=yt_ps[j0][:].rearrange("p a u m -> p a m u"),
+            )
+
+        def quantize_y(j0, tiles):
+            t0, t1 = P * j0, P * (j0 + tiles)
+            nc.vector.quantize_mx(out=y_w[:, PACK * t0 : PACK * t1].bitcast(FP8X4), scales=y_sc[:, t0:t1], in_=yt[:, PACK * t0 : PACK * t1])
             if t1 in CODE_STORES:
                 s0 = ([0] + CODE_STORES)[CODE_STORES.index(t1)]
                 nc.sync.dma_start(
@@ -348,46 +359,99 @@ def tile_neural_mass_eeg_k5_kernel(
             if t1 in SCALE_STORES:
                 s0 = ([0] + SCALE_STORES)[SCALE_STORES.index(t1)]
                 for q in range(4):
-                    queue = nc.scalar if t1 == T and q % 2 else nc.sync
+                    queue = nc.scalar if t1 == T and q % 2 == 0 else nc.sync
                     queue.dma_start(
                         out=out_2[0, 4 * q : 4 * q + 4, s0:t1].bitcast(I32),
                         in_=y_sc[32 * q : 32 * q + 4, s0:t1].bitcast(I32),
                     )
 
-        period = [
-            (scale_p, 1, (0,)),
-            (sigmoid, 1, (1, 1,)),
-            (stage2, 3, (1,)),
-            (stage1, 0, (0, 1,)),
-            (add_bg, 3, (1,)),
-            (turn_y, 8, ()),
-            (copy_turned, 8, ()),
-            (stage1, 0, (0, 0,)),
-            (round_y, 5, (0,)),
-            (quantize_p, 2, ()),
-            (calibrate, 3, (1,)),
-            (stage2, 3, (0,)),
-            (stage1, 0, (1, 0,)),
-            (stage1, 0, (1, 1,)),
-            (sigmoid, 0, (0, 1,)),
-            (scale_p, 1, (1,)),
-            (round_y, 4, (1,)),
-            (add_bg, 3, (0,)),
-            (sigmoid, 0, (0, 0,)),
-            (sigmoid, 0, (1, 0,)),
-            (quantize_y, 10, ()),
-            (calibrate, 3, (0,)),
-        ]
-        once = [
-            (interleave_lead, (0,), 0, 18),
-            (quantize_lead, (0,), 2, 8),
-            (interleave_lead, (1,), 1, 10),
-            (quantize_lead, (1,), 2, 3),
-        ]
-        for i in range(last + 1 + max(lag for step, lag, args in period)):
-            for place, (step, lag, args) in enumerate(period):
-                for extra, extra_args, extra_i, extra_place in once:
-                    if (extra_i, extra_place) == (i, place):
-                        extra(*extra_args)
-                if 0 <= i - lag <= last:
-                    step(i - lag, *args)
+        lead_steps = {1: [(interleave_lead, (0, "vector", 0, S))], 2: [(quantize_lead, (0,)), (interleave_lead, (1, "gpsimd", 0, S // 2))], 3: [(interleave_lead, (1, "scalar", S // 2, 3 * S // 4))], 4: [(interleave_lead, (1, "scalar", 3 * S // 4, S)), (quantize_lead, (1,))]}
+        wide = CHUNKS.count(PART)
+        units = [(c, g) for g in range(FG) for c in range(2)] + [(c, g) for c in range(2, wide) for g in range(FG)]
+        tile_slot = [max(j + STAGE2_LAG, FIRST_TILE_SLOT + 2 * j // 3) for j in range(TILES)]
+        to_copy = []
+        to_quantize = []
+        rounded = 0
+        turned = 0
+        for slot, (c, g) in enumerate(units):
+            tiles = [j for j in range(TILES) if tile_slot[j] == slot]
+            stage1(c, g, 0)
+            if slot == 1:
+                turn_gain()
+            if slot > 0:
+                scale_p(*units[slot - 1], 0)
+            for step, args in lead_steps.get(slot, []):
+                step(*args)
+            for j in tiles[:-1]:
+                stage2(j)
+                calibrate(j)
+            if tile_slot[rounded] + ROUND_LAG <= slot:
+                round_y(rounded)
+                rounded += 1
+            stage1(c, g, 1)
+            for j in tiles[-1:]:
+                stage2(j)
+            if slot > 0 and units[slot - 1][1] == FG - 1:
+                quantize_p(units[slot - 1][0], 0)
+            elif to_quantize:
+                quantize_y(*to_quantize[0])
+                to_quantize = to_quantize[1:]
+            for j in tiles[-1:]:
+                calibrate(j)
+            if to_copy:
+                copy_turned(*to_copy[0])
+                if len(to_copy) == 1:
+                    to_quantize.append((turned - 4, 4))
+                to_copy = to_copy[1:]
+            elif tile_slot[rounded] + ROUND_LAG <= slot:
+                round_y(rounded)
+                rounded += 1
+            if rounded - turned >= 4 + TURN_LAG:
+                for first in (turned, turned + 2):
+                    turn_y(first, 2)
+                    to_copy.append((first, 2))
+                turned += 4
+
+        stage1(7, 0, 0)
+        scale_p(6, 1, 0)
+        round_y(9)
+        stage1(7, 1, 0)
+        scale_p(7, 0, 0)
+        stage2(11)
+        quantize_p(6, 0)
+        calibrate(11)
+        copy_turned(6, 2)
+        stage1(8, 0, 0)
+        round_y(10)
+        scale_p(7, 1, 0)
+        stage1(8, 1, 0)
+        scale_p(8, 0, 0)
+        stage2(12)
+        quantize_p(7, 0)
+        calibrate(12)
+        round_y(11)
+        scale_p(8, 1, 0)
+        stage2(13)
+        quantize_p(8, 0)
+        stage2(14)
+        turn_y(8, 2)
+        turn_y(10, 2)
+        copy_turned(8, 2)
+        round_y(12)
+        copy_turned(10, 2)
+        quantize_y(4, 4)
+        calibrate(13)
+        round_y(13)
+        stage2(15)
+        round_on_vector(14)
+        round_on_vector(15)
+        turn_y(12, 2)
+        turn_y(14, 1, "u_ps", 3)
+        turn_y(15, 1, "u_ps", 3)
+        copy_turned(12, 2)
+        copy_turned(14, 1)
+        copy_turned(15, 1)
+        calibrate(14)
+        calibrate(15)
+        quantize_y(8, 4)
+        quantize_y(12, 4)

@@ -32,11 +32,11 @@ TURN_RUNS = [4, 4, 4, 2, 1, 1]
 WARM_PASSES = 8
 WARM_N = 256
 STAGE2_LAG = 3
-ROUND_LAG = 2
+ROUND_LAG = 1
 TURN_LAG = 0
 QUANT_Y_LAG = 2
 FIRST_TILE_SLOT = 5
-VECTOR_TILES = (13, 14, 15)
+VECTOR_TILES = (15,)
 
 
 def starts(widths):
@@ -75,13 +75,15 @@ def tile_neural_mass_eeg_k5_kernel(
         lead_sc = [kept("lead_sc%d" % g, [P, S], U8) for g in range(FG)]
         bg = [kept("bg%d" % i, [P, w // P, S], BF16) for i, w in enumerate(BG_LOADS)]
         calib_all = kept("calib_all", [P, S], BF16)
-        gain_rows = kept("gain_rows", [P, FG * P], BF16)
-        gain_ps = psum.tile([P, FG, P], BF16, name="gain_ps", tag="gain_ps", bufs=1)
+        calib_col = kept("calib_col", [P, PACK], BF16)
+        calib_f32 = kept("calib_f32", [P, PACK], F32)
+        gain_row = kept("gain_row", [FG, K_PASS], BF16)
+        gain_sq = kept("gain_sq", [P, PACK, P], F32)
+        gain_ps = psum.tile([P, BANK], F32, name="gain_ps", tag="gain_ps", bufs=1)
         zero_bf = kept("zero_bf", [P, PACK * WARM_N], BF16)
         zero_w = kept("zero_w", [P, PACK * WARM_N], U8)
         zero_sc = kept("zero_sc", [P, WARM_N], U8)
         ident = kept("ident", [P, P], F32)
-        ident_bf = kept("ident_bf", [P, P], BF16)
         warm = kept("warm", [P, 1], F32)
         y_w = kept("y_w", [P, PACK * T], U8)
         yt = kept("yt", [P, PACK * T], BF16)
@@ -129,10 +131,7 @@ def tile_neural_mass_eeg_k5_kernel(
                 nc.sync.dma_start(out=lead_raw[g][r:P:4], in_=rows[r])
 
         def load_gain():
-            nc.sync.dma_start(
-                out=gain_rows[:PACK].rearrange("t (m r) -> t m r", r=4),
-                in_=gain.rearrange("(m t r) -> t m r", t=PACK, r=4),
-            )
+            nc.scalar.dma_start(out=gain_row[:], in_=gain.rearrange("(g f) -> g f", g=FG))
 
         def load_bg(i):
             t0 = starts(BG_LOADS)[i]
@@ -175,9 +174,30 @@ def tile_neural_mass_eeg_k5_kernel(
             )
 
         def turn_gain():
-            for g in range(FG):
-                nc.tensor.transpose(gain_ps[:, g, :], gain_rows[:, P * g : P * (g + 1)], ident_bf[:])
+            for t in range(PACK):
+                nc.tensor.transpose(gain_ps[:, FG * t : FG * t + P], gain_sq[:, t, :], ident[:])
 
+        def order_gain():
+            nc.vector.tensor_copy(
+                out=gain_sq[:FG].rearrange("g t (q r) -> g t q r", r=4),
+                in_=gain_row[:].rearrange("g (q t r) -> g t q r", t=PACK, r=4),
+            )
+
+        warm_ps = psum.tile([P, WARM_N], F32, name="warm_ps", tag="e_ps", bufs=2)
+
+        def warm_up(passes):
+            for i in range(passes):
+                nc.tensor.matmul_mx(
+                    out=warm_ps[:],
+                    lhsT=zero_w[:, : PACK * P].bitcast(FP8X4),
+                    lhsT_scale=zero_sc[:, :P],
+                    rhs=zero_w[:].bitcast(FP8X4),
+                    rhs_scale=zero_sc[:],
+                    start=True,
+                    stop=True,
+                )
+
+        load_gain()
         load_rate_words(0)
         load_conn_words(0)
         zero(conn_sc_raw)
@@ -191,32 +211,21 @@ def tile_neural_mass_eeg_k5_kernel(
         load_rate_scales(0, 2, nc.sync)
         load_rate_scales(0, 3, nc.sync)
         load_conn_words(1)
-
+        make_identity(nc, ident[:])
         nc.vector.memset(zero_bf[:], 0.0)
         nc.vector.memset(warm[:], 0.0)
-        nc.vector.memset(gain_rows[:], 0.0)
+        nc.vector.memset(gain_sq[:], 0.0)
         nc.vector.quantize_mx(out=zero_w[:].bitcast(FP8X4), scales=zero_sc[:], in_=zero_bf[:])
         nc.scalar.activation(out=warm[:], in_=warm[:], func=ACT.Sigmoid)
-        load_gain()
-        make_identity(nc, ident_bf[:])
-        warm_ps = psum.tile([P, WARM_N], F32, name="warm_ps", tag="e_ps", bufs=2)
-        for i in range(WARM_PASSES):
-            nc.tensor.matmul_mx(
-                out=warm_ps[:],
-                lhsT=zero_w[:, : PACK * P].bitcast(FP8X4),
-                lhsT_scale=zero_sc[:, :P],
-                rhs=zero_w[:].bitcast(FP8X4),
-                rhs_scale=zero_sc[:],
-                start=True,
-                stop=True,
-            )
-
+        order_gain()
+        warm_up(WARM_PASSES - 3)
+        turn_gain()
+        warm_up(3)
         permute_conn_words(0, 0, 2)
         permute_conn_words(0, 2, 4)
         permute_conn_scales(0, 0, 2)
         permute_conn_scales(0, 2, 4)
         zero(rate_sc[1])
-        make_identity(nc, ident[:])
         permute_conn_scales(1, 0, 4)
         permute_conn_words(1, 0, 2)
         permute_conn_words(1, 2, 4)
@@ -231,8 +240,10 @@ def tile_neural_mass_eeg_k5_kernel(
         load_rate_words(2)
         load_bg(1)
         load_bg(2)
+        nc.sync.dma_start(out=calib_col[:], in_=calib.rearrange("(p t) -> p t", t=PACK))
 
         chunk_t0 = starts(CHUNKS)
+        calib_ps = {}
         sig = {}
         p_bf = {}
         p_w = {}
@@ -271,7 +282,7 @@ def tile_neural_mass_eeg_k5_kernel(
             per_bank = BANK // n
             if g == 0:
                 p_bf[c, h] = work.tile([P, FG, w, PACK], BF16, name="p_bf", tag="p_bf", bufs=3, align_bytes=64)
-            gains = gain_ps[:, g, :PACK]
+            gains = gain_ps[:, g : FG * PACK : FG]
             if per_bank == 1:
                 nc.vector.tensor_tensor(
                     out=p_bf[c, h][:, g].rearrange("p (m i) t -> p m t i", i=4),
@@ -297,10 +308,10 @@ def tile_neural_mass_eeg_k5_kernel(
                 in_=p_bf[c, h][:].rearrange("p g n t -> p (g n t)"),
             )
 
-        def stage2(j):
+        def stage2(j, tag="e_ps", bufs=2):
             c, off = locate(CHUNKS, P * j)
             h, a = divmod(off // P, PART // P)
-            e_ps = psum.tile([P, S], F32, name="e_ps", tag="e_ps", bufs=2)
+            e_ps = psum.tile([P, S], F32, name="e_ps", tag=tag, bufs=bufs)
             for g in range(FG):
                 nc.tensor.matmul_mx(
                     out=e_ps[:],
@@ -317,16 +328,31 @@ def tile_neural_mass_eeg_k5_kernel(
 
         def calibrate(j):
             y[j] = work.tile([P, S], F32, name="y", tag="y", bufs=6)
-            engine = nc.vector if j in VECTOR_TILES else nc.gpsimd
-            engine.tensor_tensor(out=y[j][:], in0=tsum[j][:], in1=calib_all[:], op=ALU.mult)
+            if j in VECTOR_TILES:
+                nc.vector.tensor_tensor(
+                    out=y[j][:].rearrange("p (m t) -> p m t", t=PACK),
+                    in0=tsum[j][:].rearrange("p (m t) -> p m t", t=PACK),
+                    in1=calib_ps["tile"][:].rearrange("p t m -> p m t"),
+                    op=ALU.mult,
+                )
+            else:
+                nc.gpsimd.tensor_tensor(out=y[j][:], in0=tsum[j][:], in1=calib_all[:], op=ALU.mult)
             nc.sync.dma_start(out=out_0[P * j : P * (j + 1), :], in_=y[j][:])
+
+        def widen_calib():
+            nc.gpsimd.tensor_copy(out=calib_f32[:], in_=calib_col[:])
+
+        def spread_calib():
+            calib_ps["tile"] = psum.tile([P, PACK, P], F32, name="calib_ps", tag="u_ps", bufs=3)
+            for t in range(PACK):
+                nc.tensor.transpose(calib_ps["tile"][:, t, :], calib_f32[:, t : t + 1].to_broadcast([P, P]), ident[:])
 
         def round_on_vector(j):
             y_bf[j] = work.tile([P, 2, P, 2], BF16, name="y_bf", tag="y_bf", bufs=8)
             nc.vector.tensor_tensor(
                 out=y_bf[j][:],
                 in0=tsum[j][:].rearrange("p (m u e) -> p u m e", u=2, e=2),
-                in1=calib_all[:].rearrange("p (m u e) -> p u m e", u=2, e=2),
+                in1=calib_ps["tile"][:].rearrange("p (u e) m -> p u m e", u=2),
                 op=ALU.mult,
             )
 
@@ -365,7 +391,7 @@ def tile_neural_mass_eeg_k5_kernel(
                         in_=y_sc[32 * q : 32 * q + 4, s0:t1].bitcast(I32),
                     )
 
-        lead_steps = {1: [(interleave_lead, (0, "vector", 0, S))], 2: [(quantize_lead, (0,)), (interleave_lead, (1, "gpsimd", 0, S // 2))], 3: [(interleave_lead, (1, "scalar", S // 2, 3 * S // 4))], 4: [(interleave_lead, (1, "scalar", 3 * S // 4, S)), (quantize_lead, (1,))]}
+        lead_steps = {1: [(interleave_lead, (0, "gpsimd", 0, S))], 2: [(interleave_lead, (1, "vector", 0, S // 2)), (interleave_lead, (1, "scalar", S // 2, 3 * S // 4)), (quantize_lead, (0,))], 3: [(interleave_lead, (1, "scalar", 3 * S // 4, S)), (quantize_lead, (1,))], 11: [(widen_calib, ())]}
         wide = CHUNKS.count(PART)
         units = [(c, g) for g in range(FG) for c in range(2)] + [(c, g) for c in range(2, wide) for g in range(FG)]
         tile_slot = [max(j + STAGE2_LAG, FIRST_TILE_SLOT + 2 * j // 3) for j in range(TILES)]
@@ -376,8 +402,6 @@ def tile_neural_mass_eeg_k5_kernel(
         for slot, (c, g) in enumerate(units):
             tiles = [j for j in range(TILES) if tile_slot[j] == slot]
             stage1(c, g, 0)
-            if slot == 1:
-                turn_gain()
             if slot > 0:
                 scale_p(*units[slot - 1], 0)
             for step, args in lead_steps.get(slot, []):
@@ -385,7 +409,12 @@ def tile_neural_mass_eeg_k5_kernel(
             for j in tiles[:-1]:
                 stage2(j)
                 calibrate(j)
-            if tile_slot[rounded] + ROUND_LAG <= slot:
+            if to_copy:
+                for pair in to_copy:
+                    copy_turned(*pair)
+                to_quantize.append((turned - 4, 4))
+                to_copy = []
+            elif tile_slot[rounded] + ROUND_LAG < slot:
                 round_y(rounded)
                 rounded += 1
             stage1(c, g, 1)
@@ -398,60 +427,54 @@ def tile_neural_mass_eeg_k5_kernel(
                 to_quantize = to_quantize[1:]
             for j in tiles[-1:]:
                 calibrate(j)
-            if to_copy:
-                copy_turned(*to_copy[0])
-                if len(to_copy) == 1:
-                    to_quantize.append((turned - 4, 4))
-                to_copy = to_copy[1:]
-            elif tile_slot[rounded] + ROUND_LAG <= slot:
-                round_y(rounded)
-                rounded += 1
-            if rounded - turned >= 4 + TURN_LAG:
+            if rounded - turned >= 4:
                 for first in (turned, turned + 2):
                     turn_y(first, 2)
                     to_copy.append((first, 2))
                 turned += 4
+            if tile_slot[rounded] + ROUND_LAG <= slot:
+                round_y(rounded)
+                rounded += 1
 
         stage1(7, 0, 0)
         scale_p(6, 1, 0)
-        round_y(9)
         stage1(7, 1, 0)
         scale_p(7, 0, 0)
         stage2(11)
         quantize_p(6, 0)
         calibrate(11)
-        copy_turned(6, 2)
-        stage1(8, 0, 0)
         round_y(10)
+        stage1(8, 0, 0)
         scale_p(7, 1, 0)
         stage1(8, 1, 0)
         scale_p(8, 0, 0)
-        stage2(12)
         quantize_p(7, 0)
+        scale_p(8, 1, 0)
+        stage2(12)
+        quantize_p(8, 0)
         calibrate(12)
         round_y(11)
-        scale_p(8, 1, 0)
         stage2(13)
-        quantize_p(8, 0)
-        stage2(14)
+        spread_calib()
+        stage2(14, "u_ps", 3)
         turn_y(8, 2)
         turn_y(10, 2)
         copy_turned(8, 2)
-        round_y(12)
         copy_turned(10, 2)
-        quantize_y(4, 4)
+        round_y(12)
+        round_on_vector(13)
         calibrate(13)
-        round_y(13)
-        stage2(15)
+        stage2(15, "u_ps", 3)
         round_on_vector(14)
+        calibrate(14)
         round_on_vector(15)
         turn_y(12, 2)
-        turn_y(14, 1, "u_ps", 3)
-        turn_y(15, 1, "u_ps", 3)
+        turn_y(14, 1)
+        turn_y(15, 1, "e_ps", 2)
         copy_turned(12, 2)
         copy_turned(14, 1)
         copy_turned(15, 1)
-        calibrate(14)
         calibrate(15)
         quantize_y(8, 4)
-        quantize_y(12, 4)
+        quantize_y(12, 3)
+        quantize_y(15, 1)

@@ -22,6 +22,7 @@ KP = K // K_PASS
 FG = F // K_PASS
 BANK = 512
 PART = 256
+RUN = 4
 TILES = T // P
 CHUNKS = [256] * 7 + [128] * 2
 RATE_LOADS = [512, 512, 1024]
@@ -273,30 +274,21 @@ def tile_neural_mass_eeg_k5_kernel(
                         stop=(k == KP - 1),
                     )
             if u == 0:
-                sig[c, g] = work.tile([P, PACK // per_bank, n, per_bank], F32, name="sig", tag="sig", bufs=4, align_bytes=64)
-            nc.scalar.activation(out=sig[c, g][:, u], in_=u_ps[:].rearrange("p e n -> p n e"), func=ACT.Sigmoid)
+                sig[c, g] = work.tile([P, PACK, n], F32, name="sig", tag="sig", bufs=4, align_bytes=64)
+            nc.scalar.activation(out=sig[c, g][:, u * per_bank : (u + 1) * per_bank, :], in_=u_ps[:], func=ACT.Sigmoid)
 
         def scale_p(c, g, h):
             n = CHUNKS[c]
             w = min(n, PART)
-            per_bank = BANK // n
             if g == 0:
                 p_bf[c, h] = work.tile([P, FG, w, PACK], BF16, name="p_bf", tag="p_bf", bufs=3, align_bytes=64)
             gains = gain_ps[:, g : FG * PACK : FG]
-            if per_bank == 1:
-                nc.vector.tensor_tensor(
-                    out=p_bf[c, h][:, g].rearrange("p (m i) t -> p m t i", i=4),
-                    in0=sig[c, g][:, :, w * h : w * (h + 1), 0].rearrange("p t (m i) -> p m t i", i=4),
-                    in1=gains.unsqueeze(1).unsqueeze(3).to_broadcast([P, w // 4, PACK, 4]),
-                    op=ALU.mult,
-                )
-            else:
-                nc.vector.tensor_tensor(
-                    out=p_bf[c, h][:, g].rearrange("p n (u e) -> p n u e", e=per_bank),
-                    in0=sig[c, g][:].rearrange("p u n e -> p n u e"),
-                    in1=gains.rearrange("p (u e) -> p u e", e=per_bank).unsqueeze(1).to_broadcast([P, w, PACK // per_bank, per_bank]),
-                    op=ALU.mult,
-                )
+            nc.vector.tensor_tensor(
+                out=p_bf[c, h][:, g].rearrange("p (m i) t -> p m t i", i=RUN),
+                in0=sig[c, g][:, :, w * h : w * (h + 1)].rearrange("p t (m i) -> p m t i", i=RUN),
+                in1=gains.unsqueeze(1).unsqueeze(3).to_broadcast([P, w // RUN, PACK, RUN]),
+                op=ALU.mult,
+            )
 
         def quantize_p(c, h):
             w = min(CHUNKS[c], PART)

@@ -25,19 +25,19 @@ PART = 256
 RUN = 4
 TILES = T // P
 CHUNKS = [256] * 7 + [128] * 2
-RATE_LOADS = [512, 512, 1024]
+RATE_LOADS = [256, 256, 512, 1024]
 BG_LOADS = [512, 512, 1024]
-CODE_STORES = [512, 1024, 1536, 2048]
-SCALE_STORES = [2048]
+CODE_STORES = [512, 1024, 1536, 1792, 2048]
+SCALE_STORES = [1024, 2048]
 TURN_RUNS = [4, 4, 4, 2, 1, 1]
-WARM_PASSES = 8
+WARM_PASSES = 10
 WARM_N = 256
 STAGE2_LAG = 3
 ROUND_LAG = 1
 TURN_LAG = 0
 QUANT_Y_LAG = 2
-FIRST_TILE_SLOT = 5
-VECTOR_TILES = (15,)
+FIRST_TILE_SLOT = 6
+VECTOR_TILES = (13, 14, 15)
 
 
 def starts(widths):
@@ -76,8 +76,6 @@ def tile_neural_mass_eeg_k5_kernel(
         lead_sc = [kept("lead_sc%d" % g, [P, S], U8) for g in range(FG)]
         bg = [kept("bg%d" % i, [P, w // P, S], BF16) for i, w in enumerate(BG_LOADS)]
         calib_all = kept("calib_all", [P, S], BF16)
-        calib_col = kept("calib_col", [P, PACK], BF16)
-        calib_f32 = kept("calib_f32", [P, PACK], F32)
         gain_row = kept("gain_row", [FG, K_PASS], BF16)
         gain_sq = kept("gain_sq", [P, PACK, P], F32)
         gain_ps = psum.tile([P, BANK], F32, name="gain_ps", tag="gain_ps", bufs=1)
@@ -211,6 +209,7 @@ def tile_neural_mass_eeg_k5_kernel(
         load_rate_scales(0, 1, nc.scalar)
         load_rate_scales(0, 2, nc.sync)
         load_rate_scales(0, 3, nc.sync)
+        load_rate_words(1)
         load_conn_words(1)
         make_identity(nc, ident[:])
         nc.vector.memset(zero_bf[:], 0.0)
@@ -219,9 +218,9 @@ def tile_neural_mass_eeg_k5_kernel(
         nc.vector.quantize_mx(out=zero_w[:].bitcast(FP8X4), scales=zero_sc[:], in_=zero_bf[:])
         nc.scalar.activation(out=warm[:], in_=warm[:], func=ACT.Sigmoid)
         order_gain()
-        warm_up(WARM_PASSES - 3)
+        warm_up(WARM_PASSES - 5)
         turn_gain()
-        warm_up(3)
+        warm_up(5)
         permute_conn_words(0, 0, 2)
         permute_conn_words(0, 2, 4)
         permute_conn_scales(0, 0, 2)
@@ -233,18 +232,16 @@ def tile_neural_mass_eeg_k5_kernel(
 
         load_lead(0)
         load_lead(1)
-        load_rate_words(1)
+        load_rate_words(2)
         for q in range(4):
             load_rate_scales(1, q, nc.sync)
         load_bg(0)
         nc.sync.dma_start(out=calib_all[:], in_=calib.partition_broadcast(P))
-        load_rate_words(2)
+        load_rate_words(3)
         load_bg(1)
         load_bg(2)
-        nc.sync.dma_start(out=calib_col[:], in_=calib.rearrange("(p t) -> p t", t=PACK))
 
         chunk_t0 = starts(CHUNKS)
-        calib_ps = {}
         sig = {}
         p_bf = {}
         p_w = {}
@@ -320,31 +317,16 @@ def tile_neural_mass_eeg_k5_kernel(
 
         def calibrate(j):
             y[j] = work.tile([P, S], F32, name="y", tag="y", bufs=6)
-            if j in VECTOR_TILES:
-                nc.vector.tensor_tensor(
-                    out=y[j][:].rearrange("p (m t) -> p m t", t=PACK),
-                    in0=tsum[j][:].rearrange("p (m t) -> p m t", t=PACK),
-                    in1=calib_ps["tile"][:].rearrange("p t m -> p m t"),
-                    op=ALU.mult,
-                )
-            else:
-                nc.gpsimd.tensor_tensor(out=y[j][:], in0=tsum[j][:], in1=calib_all[:], op=ALU.mult)
+            engine = nc.vector if j in VECTOR_TILES else nc.gpsimd
+            engine.tensor_tensor(out=y[j][:], in0=tsum[j][:], in1=calib_all[:], op=ALU.mult)
             nc.sync.dma_start(out=out_0[P * j : P * (j + 1), :], in_=y[j][:])
-
-        def widen_calib():
-            nc.gpsimd.tensor_copy(out=calib_f32[:], in_=calib_col[:])
-
-        def spread_calib():
-            calib_ps["tile"] = psum.tile([P, PACK, P], F32, name="calib_ps", tag="u_ps", bufs=3)
-            for t in range(PACK):
-                nc.tensor.transpose(calib_ps["tile"][:, t, :], calib_f32[:, t : t + 1].to_broadcast([P, P]), ident[:])
 
         def round_on_vector(j):
             y_bf[j] = work.tile([P, 2, P, 2], BF16, name="y_bf", tag="y_bf", bufs=8)
             nc.vector.tensor_tensor(
                 out=y_bf[j][:],
                 in0=tsum[j][:].rearrange("p (m u e) -> p u m e", u=2, e=2),
-                in1=calib_ps["tile"][:].rearrange("p (u e) m -> p u m e", u=2),
+                in1=calib_all[:].rearrange("p (m u e) -> p u m e", u=2, e=2),
                 op=ALU.mult,
             )
 
@@ -383,10 +365,10 @@ def tile_neural_mass_eeg_k5_kernel(
                         in_=y_sc[32 * q : 32 * q + 4, s0:t1].bitcast(I32),
                     )
 
-        lead_steps = {1: [(interleave_lead, (0, "gpsimd", 0, S))], 2: [(interleave_lead, (1, "vector", 0, S // 2)), (interleave_lead, (1, "scalar", S // 2, 3 * S // 4)), (quantize_lead, (0,))], 3: [(interleave_lead, (1, "scalar", 3 * S // 4, S)), (quantize_lead, (1,))], 11: [(widen_calib, ())]}
+        lead_steps = {1: [(interleave_lead, (0, "gpsimd", 0, S))], 2: [(interleave_lead, (1, "gpsimd", 0, S // 2)), (interleave_lead, (1, "scalar", S // 2, 3 * S // 4))], 3: [(interleave_lead, (1, "scalar", 3 * S // 4, S)), (quantize_lead, (0,))], 4: [(quantize_lead, (1,))]}
         wide = CHUNKS.count(PART)
         units = [(c, g) for g in range(FG) for c in range(2)] + [(c, g) for c in range(2, wide) for g in range(FG)]
-        tile_slot = [max(j + STAGE2_LAG, FIRST_TILE_SLOT + 2 * j // 3) for j in range(TILES)]
+        tile_slot = [max(j + STAGE2_LAG, FIRST_TILE_SLOT + 3 * j // 5) for j in range(TILES)]
         to_copy = []
         to_quantize = []
         rounded = 0
@@ -447,26 +429,25 @@ def tile_neural_mass_eeg_k5_kernel(
         calibrate(12)
         round_y(11)
         stage2(13)
-        spread_calib()
         stage2(14, "u_ps", 3)
         turn_y(8, 2)
         turn_y(10, 2)
         copy_turned(8, 2)
         copy_turned(10, 2)
         round_y(12)
-        round_on_vector(13)
         calibrate(13)
+        round_y(13)
         stage2(15, "u_ps", 3)
-        round_on_vector(14)
         calibrate(14)
+        round_y(14)
         round_on_vector(15)
         turn_y(12, 2)
-        turn_y(14, 1)
         turn_y(15, 1, "e_ps", 2)
+        turn_y(14, 1)
         copy_turned(12, 2)
-        copy_turned(14, 1)
         copy_turned(15, 1)
+        copy_turned(14, 1)
         calibrate(15)
         quantize_y(8, 4)
-        quantize_y(12, 3)
-        quantize_y(15, 1)
+        quantize_y(12, 2)
+        quantize_y(14, 2)

@@ -27,7 +27,7 @@ TILES = T // P
 CHUNKS = [256] * 7 + [128] * 2
 RATE_LOADS = [256, 256, 512, 1024]
 BG_LOADS = [512, 512, 1024]
-CODE_STORES = [512, 1024, 1536, 1792, 2048]
+CODE_STORES = [512, 1024, 1536, 2048]
 SCALE_STORES = [1024, 2048]
 TURN_RUNS = [4, 4, 4, 2, 1, 1]
 WARM_PASSES = 10
@@ -37,7 +37,7 @@ ROUND_LAG = 1
 TURN_LAG = 0
 QUANT_Y_LAG = 2
 FIRST_TILE_SLOT = 6
-VECTOR_TILES = (13, 14, 15)
+VECTOR_TILES = (15,)
 
 
 def starts(widths):
@@ -63,7 +63,7 @@ def tile_neural_mass_eeg_k5_kernel(
         def kept(name, shape, dtype):
             return keep.tile(shape, dtype, name=name, align_bytes=64)
 
-        rate_scale_loads = [512, T - 512]
+        rate_scale_loads = [768, T - 768]
         conn_raw = [kept("conn_raw%d" % g, [P, KP, 2 * K_PASS], U8) for g in range(FG)]
         conn_sc_raw = kept("conn_sc_raw", [P, KP, F], U8)
         conn_w = [kept("conn_w%d" % g, [P, PACK, KP, 2 * P], U8) for g in range(FG)]
@@ -76,6 +76,8 @@ def tile_neural_mass_eeg_k5_kernel(
         lead_sc = [kept("lead_sc%d" % g, [P, S], U8) for g in range(FG)]
         bg = [kept("bg%d" % i, [P, w // P, S], BF16) for i, w in enumerate(BG_LOADS)]
         calib_all = kept("calib_all", [P, S], BF16)
+        calib_col = kept("calib_col", [P, PACK], BF16)
+        calib_f32 = kept("calib_f32", [P, PACK], F32)
         gain_row = kept("gain_row", [FG, K_PASS], BF16)
         gain_sq = kept("gain_sq", [P, PACK, P], F32)
         gain_ps = psum.tile([P, BANK], F32, name="gain_ps", tag="gain_ps", bufs=1)
@@ -240,8 +242,10 @@ def tile_neural_mass_eeg_k5_kernel(
         load_rate_words(3)
         load_bg(1)
         load_bg(2)
+        nc.sync.dma_start(out=calib_col[:], in_=calib.rearrange("(p t) -> p t", t=PACK))
 
         chunk_t0 = starts(CHUNKS)
+        calib_ps = {}
         sig = {}
         p_bf = {}
         p_w = {}
@@ -317,16 +321,31 @@ def tile_neural_mass_eeg_k5_kernel(
 
         def calibrate(j):
             y[j] = work.tile([P, S], F32, name="y", tag="y", bufs=6)
-            engine = nc.vector if j in VECTOR_TILES else nc.gpsimd
-            engine.tensor_tensor(out=y[j][:], in0=tsum[j][:], in1=calib_all[:], op=ALU.mult)
+            if j in VECTOR_TILES:
+                nc.vector.tensor_tensor(
+                    out=y[j][:].rearrange("p (m t) -> p m t", t=PACK),
+                    in0=tsum[j][:].rearrange("p (m t) -> p m t", t=PACK),
+                    in1=calib_ps["tile"][:].rearrange("p t m -> p m t"),
+                    op=ALU.mult,
+                )
+            else:
+                nc.gpsimd.tensor_tensor(out=y[j][:], in0=tsum[j][:], in1=calib_all[:], op=ALU.mult)
             nc.sync.dma_start(out=out_0[P * j : P * (j + 1), :], in_=y[j][:])
+
+        def widen_calib():
+            nc.gpsimd.tensor_copy(out=calib_f32[:], in_=calib_col[:])
+
+        def spread_calib():
+            calib_ps["tile"] = psum.tile([P, PACK, P], F32, name="calib_ps", tag="u_ps", bufs=3)
+            for t in range(PACK):
+                nc.tensor.transpose(calib_ps["tile"][:, t, :], calib_f32[:, t : t + 1].to_broadcast([P, P]), ident[:])
 
         def round_on_vector(j):
             y_bf[j] = work.tile([P, 2, P, 2], BF16, name="y_bf", tag="y_bf", bufs=8)
             nc.vector.tensor_tensor(
                 out=y_bf[j][:],
                 in0=tsum[j][:].rearrange("p (m u e) -> p u m e", u=2, e=2),
-                in1=calib_all[:].rearrange("p (m u e) -> p u m e", u=2, e=2),
+                in1=calib_ps["tile"][:].rearrange("p (u e) m -> p u m e", u=2),
                 op=ALU.mult,
             )
 
@@ -365,7 +384,7 @@ def tile_neural_mass_eeg_k5_kernel(
                         in_=y_sc[32 * q : 32 * q + 4, s0:t1].bitcast(I32),
                     )
 
-        lead_steps = {1: [(interleave_lead, (0, "gpsimd", 0, S))], 2: [(interleave_lead, (1, "gpsimd", 0, S // 2)), (interleave_lead, (1, "scalar", S // 2, 3 * S // 4))], 3: [(interleave_lead, (1, "scalar", 3 * S // 4, S)), (quantize_lead, (0,))], 4: [(quantize_lead, (1,))]}
+        lead_steps = {1: [(interleave_lead, (0, "gpsimd", 0, S))], 2: [(interleave_lead, (1, "gpsimd", 0, S // 2)), (interleave_lead, (1, "scalar", S // 2, 3 * S // 4))], 3: [(interleave_lead, (1, "scalar", 3 * S // 4, S)), (quantize_lead, (0,))], 4: [(quantize_lead, (1,))], 11: [(widen_calib, ())]}
         wide = CHUNKS.count(PART)
         units = [(c, g) for g in range(FG) for c in range(2)] + [(c, g) for c in range(2, wide) for g in range(FG)]
         tile_slot = [max(j + STAGE2_LAG, FIRST_TILE_SLOT + 3 * j // 5) for j in range(TILES)]
@@ -380,8 +399,11 @@ def tile_neural_mass_eeg_k5_kernel(
                 scale_p(*units[slot - 1], 0)
             for step, args in lead_steps.get(slot, []):
                 step(*args)
+            whole = slot > 0 and units[slot - 1][1] == FG - 1
             for j in tiles[:-1]:
                 stage2(j)
+                if whole:
+                    quantize_p(units[slot - 1][0], 0)
                 calibrate(j)
             if to_copy:
                 for pair in to_copy:
@@ -394,9 +416,9 @@ def tile_neural_mass_eeg_k5_kernel(
             stage1(c, g, 1)
             for j in tiles[-1:]:
                 stage2(j)
-            if slot > 0 and units[slot - 1][1] == FG - 1:
+            if whole and len(tiles) < 2:
                 quantize_p(units[slot - 1][0], 0)
-            elif to_quantize:
+            elif to_quantize and len(tiles) < 2:
                 quantize_y(*to_quantize[0])
                 to_quantize = to_quantize[1:]
             for j in tiles[-1:]:
@@ -429,25 +451,26 @@ def tile_neural_mass_eeg_k5_kernel(
         calibrate(12)
         round_y(11)
         stage2(13)
+        spread_calib()
         stage2(14, "u_ps", 3)
         turn_y(8, 2)
         turn_y(10, 2)
         copy_turned(8, 2)
         copy_turned(10, 2)
         round_y(12)
+        round_on_vector(13)
         calibrate(13)
-        round_y(13)
         stage2(15, "u_ps", 3)
+        round_on_vector(14)
         calibrate(14)
-        round_y(14)
         round_on_vector(15)
         turn_y(12, 2)
-        turn_y(15, 1, "e_ps", 2)
         turn_y(14, 1)
+        turn_y(15, 1, "e_ps", 2)
         copy_turned(12, 2)
-        copy_turned(15, 1)
         copy_turned(14, 1)
+        copy_turned(15, 1)
         calibrate(15)
         quantize_y(8, 4)
-        quantize_y(12, 2)
-        quantize_y(14, 2)
+        quantize_y(12, 3)
+        quantize_y(15, 1)

@@ -22,6 +22,7 @@ KP = K // K_PASS
 FG = F // K_PASS
 BANK = 512
 PART = 256
+SPAN = 256
 RUN = 4
 TILES = T // P
 CHUNKS = [256] * 7 + [128] * 2
@@ -63,17 +64,22 @@ def tile_neural_mass_eeg_k5_kernel(
         def kept(name, shape, dtype):
             return keep.tile(shape, dtype, name=name, align_bytes=64)
 
+        def placed(pool, name, shape, start, **kw):
+            size = shape[1] * shape[2]
+            tile = pool.tile([P, size + SPAN], U8, name=name, align_bytes=SPAN, **kw)
+            return tile[:, start : start + size].rearrange("p (a b) -> p a b", a=shape[1])
+
         rate_scale_loads = [768, T - 768]
         conn_raw = [kept("conn_raw%d" % g, [P, KP, 2 * K_PASS], U8) for g in range(FG)]
         conn_sc_raw = kept("conn_sc_raw", [P, KP, F], U8)
-        conn_w = [kept("conn_w%d" % g, [P, PACK, KP, 2 * P], U8) for g in range(FG)]
-        conn_sc = [kept("conn_sc%d" % g, [P, PACK, KP, P], U8) for g in range(FG)]
-        rate_w = [kept("rate_w%d" % i, [P, KP, 2 * w], U8) for i, w in enumerate(RATE_LOADS)]
-        rate_sc = [kept("rate_sc%d" % i, [P, KP, w], U8) for i, w in enumerate(rate_scale_loads)]
+        conn_w = [placed(keep, "conn_w%d" % g, [P, PACK, KP * 2 * P], 0).rearrange("p t (k c) -> p t k c", k=KP) for g in range(FG)]
+        conn_sc = [placed(keep, "conn_sc%d" % g, [P, PACK, KP * P], 64).rearrange("p t (k c) -> p t k c", k=KP) for g in range(FG)]
+        rate_w = [placed(keep, "rate_w%d" % i, [P, KP, 2 * w], 128) for i, w in enumerate(RATE_LOADS)]
+        rate_sc = [placed(keep, "rate_sc%d" % i, [P, KP, w], 192) for i, w in enumerate(rate_scale_loads)]
         lead_raw = [kept("lead_raw%d" % g, [P, PACK, S], BF16) for g in range(FG)]
         lead_il = [kept("lead_il%d" % g, [P, S, PACK], BF16) for g in range(FG)]
-        lead_w = [kept("lead_w%d" % g, [P, PACK * S], U8) for g in range(FG)]
-        lead_sc = [kept("lead_sc%d" % g, [P, S], U8) for g in range(FG)]
+        lead_w = [placed(keep, "lead_w%d" % g, [P, 1, PACK * S], 128)[:, 0, :] for g in range(FG)]
+        lead_sc = [placed(keep, "lead_sc%d" % g, [P, 1, S], 192)[:, 0, :] for g in range(FG)]
         bg = [kept("bg%d" % i, [P, w // P, S], BF16) for i, w in enumerate(BG_LOADS)]
         calib_all = kept("calib_all", [P, S], BF16)
         calib_col = kept("calib_col", [P, PACK], BF16)
@@ -293,8 +299,8 @@ def tile_neural_mass_eeg_k5_kernel(
 
         def quantize_p(c, h):
             w = min(CHUNKS[c], PART)
-            p_w[c, h] = work.tile([P, FG, PACK * w], U8, name="p_w", tag="p_w", bufs=4, align_bytes=64)
-            p_sc[c, h] = work.tile([P, FG, w], U8, name="p_sc", tag="p_sc", bufs=4, align_bytes=64)
+            p_w[c, h] = placed(work, "p_w", [P, FG, PACK * w], 0, tag="p_w", bufs=4)
+            p_sc[c, h] = placed(work, "p_sc", [P, FG, w], 64, tag="p_sc", bufs=4)
             nc.vector.quantize_mx(
                 out=p_w[c, h][:].rearrange("p g w -> p (g w)").bitcast(FP8X4),
                 scales=p_sc[c, h][:].rearrange("p g n -> p (g n)"),

@@ -390,7 +390,7 @@ def tile_neural_mass_eeg_k5_kernel(
                         in_=y_sc[32 * q : 32 * q + 4, s0:t1].bitcast(I32),
                     )
 
-        lead_steps = {1: [(interleave_lead, (0, "gpsimd", 0, S))], 2: [(interleave_lead, (1, "gpsimd", 0, S // 2)), (interleave_lead, (1, "scalar", S // 2, 3 * S // 4))], 3: [(interleave_lead, (1, "scalar", 3 * S // 4, S)), (quantize_lead, (0,))], 4: [(quantize_lead, (1,))], 11: [(widen_calib, ())]}
+        lead_steps = {1: [(interleave_lead, (0, "gpsimd", 0, 3 * S // 4))], 2: [(interleave_lead, (0, "scalar", 3 * S // 4, S)), (interleave_lead, (1, "vector", 0, S // 2))], 3: [(interleave_lead, (1, "scalar", S // 2, 3 * S // 4)), (quantize_lead, (0,))], 4: [(interleave_lead, (1, "scalar", 3 * S // 4, S)), (quantize_lead, (1,))], 11: [(widen_calib, ())]}
         wide = CHUNKS.count(PART)
         units = [(c, g) for g in range(FG) for c in range(2)] + [(c, g) for c in range(2, wide) for g in range(FG)]
         tile_slot = [max(j + STAGE2_LAG, FIRST_TILE_SLOT + 3 * j // 5) for j in range(TILES)]

@@ -120,16 +120,16 @@ def tile_neural_mass_eeg_k5_kernel(
         def load_rate_scales(i, q, queue):
             t0 = starts(rate_scale_loads)[i]
             queue.dma_start(
-                out=rate_sc[i][32 * q : 32 * q + 4].bitcast(I32),
-                in_=rate_scales32[:, 4 * q : 4 * q + 4, t0 // 4 : (t0 + rate_scale_loads[i]) // 4].rearrange(
+                out=rate_sc[i][q:P:32].bitcast(I32),
+                in_=rate_scales32[:, q:16:4, t0 // 4 : (t0 + rate_scale_loads[i]) // 4].rearrange(
                     "k r c -> r k c"
                 ),
             )
 
         def load_conn_scales(q, queue):
             queue.dma_start(
-                out=conn_sc_raw[32 * q : 32 * q + 4].bitcast(I32),
-                in_=conn_scales32[:, 4 * q : 4 * q + 4, :].rearrange("k r c -> r k c"),
+                out=conn_sc_raw[q:P:32].bitcast(I32),
+                in_=conn_scales32[:, q:16:4, :].rearrange("k r c -> r k c"),
             )
 
         def load_lead(g):
@@ -386,8 +386,8 @@ def tile_neural_mass_eeg_k5_kernel(
                 for q in range(4):
                     queue = nc.scalar if t1 == T and q % 2 == 0 else nc.sync
                     queue.dma_start(
-                        out=out_2[0, 4 * q : 4 * q + 4, s0:t1].bitcast(I32),
-                        in_=y_sc[32 * q : 32 * q + 4, s0:t1].bitcast(I32),
+                        out=out_2[0, q:16:4, s0:t1].bitcast(I32),
+                        in_=y_sc[q:P:32, s0:t1].bitcast(I32),
                     )
 
         lead_steps = {1: [(interleave_lead, (0, "gpsimd", 0, 3 * S // 4))], 2: [(interleave_lead, (0, "scalar", 3 * S // 4, S)), (interleave_lead, (1, "vector", 0, S // 2))], 3: [(interleave_lead, (1, "scalar", S // 2, 3 * S // 4)), (quantize_lead, (0,))], 4: [(interleave_lead, (1, "scalar", 3 * S // 4, S)), (quantize_lead, (1,))], 11: [(widen_calib, ())]}

@@ -182,7 +182,7 @@ def tile_neural_mass_eeg_k5_kernel(
 
         def turn_gain():
             for t in range(PACK):
-                nc.tensor.transpose(gain_ps[:, FG * t : FG * t + P], gain_sq[:, t, :], ident[:])
+                nc.tensor.transpose(gain_ps[:, t:BANK:PACK], gain_sq[:, t, :], ident[:])
 
         def order_gain():
             nc.vector.tensor_copy(
@@ -281,19 +281,20 @@ def tile_neural_mass_eeg_k5_kernel(
                         stop=(k == KP - 1),
                     )
             if u == 0:
-                sig[c, g] = work.tile([P, PACK, n], F32, name="sig", tag="sig", bufs=4, align_bytes=64)
-            nc.scalar.activation(out=sig[c, g][:, u * per_bank : (u + 1) * per_bank, :], in_=u_ps[:], func=ACT.Sigmoid)
+                sig[c, g] = work.tile([P, PACK // per_bank, n, per_bank], F32, name="sig", tag="sig", bufs=4, align_bytes=64)
+            nc.scalar.activation(out=sig[c, g][:, u], in_=u_ps[:].rearrange("p e n -> p n e"), func=ACT.Sigmoid)
 
         def scale_p(c, g, h):
             n = CHUNKS[c]
             w = min(n, PART)
             if g == 0:
                 p_bf[c, h] = work.tile([P, FG, w, PACK], BF16, name="p_bf", tag="p_bf", bufs=3, align_bytes=64)
-            gains = gain_ps[:, g : FG * PACK : FG]
+            per_bank = BANK // n
+            gains = gain_ps[:, PACK * g : PACK * (g + 1)].rearrange("p (u e) -> p u e", e=per_bank)
             nc.vector.tensor_tensor(
-                out=p_bf[c, h][:, g].rearrange("p (m i) t -> p m t i", i=RUN),
-                in0=sig[c, g][:, :, w * h : w * (h + 1)].rearrange("p t (m i) -> p m t i", i=RUN),
-                in1=gains.unsqueeze(1).unsqueeze(3).to_broadcast([P, w // RUN, PACK, RUN]),
+                out=p_bf[c, h][:, g].rearrange("p n (u e) -> p n u e", e=per_bank),
+                in0=sig[c, g][:].rearrange("p u n e -> p n u e"),
+                in1=gains.unsqueeze(1).to_broadcast([P, w, PACK // per_bank, per_bank]),
                 op=ALU.mult,
             )
 

@@ -87,6 +87,7 @@ def tile_neural_mass_eeg_k5_kernel(
         gain_row = kept("gain_row", [FG, K_PASS], BF16)
         gain_sq = kept("gain_sq", [P, PACK, P], F32)
         gain_ps = psum.tile([P, BANK], F32, name="gain_ps", tag="gain_ps", bufs=1)
+        gain_sb = kept("gain_sb", [P, FG * PACK], F32)
         zero_bf = kept("zero_bf", [P, PACK * WARM_N], BF16)
         zero_w = kept("zero_w", [P, PACK * WARM_N], U8)
         zero_sc = kept("zero_sc", [P, WARM_N], U8)
@@ -254,6 +255,7 @@ def tile_neural_mass_eeg_k5_kernel(
         calib_ps = {}
         sig = {}
         p_bf = {}
+        p_slot = {}
         p_w = {}
         p_sc = {}
         e_ps = {}
@@ -281,14 +283,14 @@ def tile_neural_mass_eeg_k5_kernel(
                         stop=(k == KP - 1),
                     )
             if u == 0:
-                sig[c, g] = work.tile([P, PACK // per_bank, n, per_bank], F32, name="sig", tag="sig", bufs=4, align_bytes=64)
+                sig[c, g] = work.tile([P, PACK // per_bank, n, per_bank], F32, name="sig", tag="sig", bufs=6, align_bytes=64)
             nc.scalar.activation(out=sig[c, g][:, u], in_=u_ps[:].rearrange("p e n -> p n e"), func=ACT.Sigmoid)
 
         def scale_p(c, g, h):
             n = CHUNKS[c]
             w = min(n, PART)
-            if g == 0:
-                p_bf[c, h] = work.tile([P, FG, w, PACK], BF16, name="p_bf", tag="p_bf", bufs=3, align_bytes=64)
+            if (c, h) not in p_bf:
+                p_bf[c, h] = work.tile([P, FG, w, PACK], BF16, name="p_bf", tag="p_bf", bufs=4, align_bytes=64)
             per_bank = BANK // n
             gains = gain_ps[:, PACK * g : PACK * (g + 1)].rearrange("p (u e) -> p u e", e=per_bank)
             nc.vector.tensor_tensor(
@@ -296,6 +298,23 @@ def tile_neural_mass_eeg_k5_kernel(
                 in0=sig[c, g][:].rearrange("p u n e -> p n u e"),
                 in1=gains.unsqueeze(1).to_broadcast([P, w, PACK // per_bank, per_bank]),
                 op=ALU.mult,
+            )
+
+        def copy_gains():
+            nc.scalar.copy(out=gain_sb[:], in_=gain_ps[:, : FG * PACK])
+
+        def scale_slots(c, t0, t1):
+            if t0 == 0:
+                p_slot[c] = work.tile([P, PACK, PART], BF16, name="p_slot", tag="p_slot", bufs=1, align_bytes=64)
+            for t in range(t0, t1):
+                nc.scalar.activation(out=p_slot[c][:, t, :], in_=sig[c, 0][:, t // 2, :, t % 2], func=ACT.Copy, scale=gain_sb[:, t : t + 1])
+
+        def interleave_p(c, n0, n1):
+            if (c, 0) not in p_bf:
+                p_bf[c, 0] = work.tile([P, FG, PART, PACK], BF16, name="p_bf", tag="p_bf", bufs=4, align_bytes=64)
+            nc.scalar.copy(
+                out=p_bf[c, 0][:, 0, n0:n1].rearrange("p (m i) t -> p m t i", i=RUN),
+                in_=p_slot[c][:, :, n0:n1].rearrange("p t (m i) -> p m t i", i=RUN),
             )
 
         def quantize_p(c, h):
@@ -391,7 +410,20 @@ def tile_neural_mass_eeg_k5_kernel(
                         in_=y_sc[q:P:32, s0:t1].bitcast(I32),
                     )
 
-        lead_steps = {1: [(interleave_lead, (0, "gpsimd", 0, 3 * S // 4))], 2: [(interleave_lead, (0, "scalar", 3 * S // 4, S)), (interleave_lead, (1, "vector", 0, S // 2))], 3: [(interleave_lead, (1, "scalar", S // 2, 3 * S // 4)), (quantize_lead, (0,))], 4: [(interleave_lead, (1, "scalar", 3 * S // 4, S)), (quantize_lead, (1,))], 11: [(widen_calib, ())]}
+        half = PART // 2
+        before_gain = {1: [(interleave_lead, (0, "vector", 0, S)), (interleave_lead, (1, "gpsimd", 0, S))]}
+        late_steps = {6: [(interleave_p, (2, 0, PART))]}
+        lead_steps = {
+            0: [(copy_gains, ())],
+            2: [(scale_slots, (1, 0, 2))],
+            3: [(scale_slots, (1, 2, 4)), (quantize_lead, (0,))],
+            4: [(interleave_p, (1, 0, half)), (quantize_lead, (1,)), (quantize_p, (0, 0))],
+            5: [(interleave_p, (1, half, PART))],
+            6: [(scale_slots, (2, 0, 4))],
+            11: [(widen_calib, ())],
+        }
+        on_scalar = ((1, 0), (2, 0))
+        quantize_slot = {6: 1, 7: 2}
         wide = CHUNKS.count(PART)
         units = [(c, g) for g in range(FG) for c in range(2)] + [(c, g) for c in range(2, wide) for g in range(FG)]
         tile_slot = [max(j + STAGE2_LAG, FIRST_TILE_SLOT + 3 * j // 5) for j in range(TILES)]
@@ -402,15 +434,18 @@ def tile_neural_mass_eeg_k5_kernel(
         for slot, (c, g) in enumerate(units):
             tiles = [j for j in range(TILES) if tile_slot[j] == slot]
             stage1(c, g, 0)
-            if slot > 0:
+            for step, args in before_gain.get(slot, []):
+                step(*args)
+            if slot > 0 and units[slot - 1] not in on_scalar:
                 scale_p(*units[slot - 1], 0)
             for step, args in lead_steps.get(slot, []):
                 step(*args)
-            whole = slot > 0 and units[slot - 1][1] == FG - 1
+            whole = slot > FIRST_TILE_SLOT + 1 and units[slot - 1][1] == FG - 1 or slot in quantize_slot
+            chunk = quantize_slot.get(slot, units[slot - 1][0])
             for j in tiles[:-1]:
                 stage2(j)
                 if whole:
-                    quantize_p(units[slot - 1][0], 0)
+                    quantize_p(chunk, 0)
                 calibrate(j)
             if to_copy:
                 for pair in to_copy:
@@ -421,10 +456,12 @@ def tile_neural_mass_eeg_k5_kernel(
                 round_y(rounded)
                 rounded += 1
             stage1(c, g, 1)
+            for step, args in late_steps.get(slot, []):
+                step(*args)
             for j in tiles[-1:]:
                 stage2(j)
             if whole and len(tiles) < 2:
-                quantize_p(units[slot - 1][0], 0)
+                quantize_p(chunk, 0)
             elif to_quantize and len(tiles) < 2:
                 quantize_y(*to_quantize[0])
                 to_quantize = to_quantize[1:]

@@ -264,12 +264,12 @@ def tile_neural_mass_eeg_k5_kernel(
         y_bf = {}
         yt_ps = {}
 
-        def stage1(c, g, u):
+        def stage1(c, g, u, tag="u_ps", bufs=3):
             n = CHUNKS[c]
             per_bank = BANK // n
             i, off = locate(RATE_LOADS, chunk_t0[c])
             j, soff = locate(rate_scale_loads, chunk_t0[c])
-            u_ps = psum.tile([P, per_bank, n], F32, name="u_ps", tag="u_ps", bufs=3)
+            u_ps = psum.tile([P, per_bank, n], F32, name="u_ps", tag=tag, bufs=bufs)
             for e in range(per_bank):
                 t = u * per_bank + e
                 for k in range(KP):
@@ -411,19 +411,19 @@ def tile_neural_mass_eeg_k5_kernel(
                     )
 
         half = PART // 2
-        before_gain = {1: [(interleave_lead, (0, "vector", 0, S)), (interleave_lead, (1, "gpsimd", 0, S))]}
+        before_gain = {}
         late_steps = {6: [(interleave_p, (2, 0, PART))]}
         lead_steps = {
             0: [(copy_gains, ())],
-            2: [(scale_slots, (1, 0, 2))],
-            3: [(scale_slots, (1, 2, 4)), (quantize_lead, (0,))],
-            4: [(interleave_p, (1, 0, half)), (quantize_lead, (1,)), (quantize_p, (0, 0))],
-            5: [(interleave_p, (1, half, PART))],
+            1: [(interleave_lead, (0, "gpsimd", 0, 3 * S // 4))],
+            2: [(interleave_lead, (0, "scalar", 3 * S // 4, S)), (interleave_lead, (1, "vector", 0, S // 2))],
+            3: [(interleave_lead, (1, "scalar", S // 2, 3 * S // 4)), (quantize_lead, (0,)), (quantize_p, (0, 0))],
+            4: [(interleave_lead, (1, "scalar", 3 * S // 4, S)), (quantize_lead, (1,)), (quantize_p, (1, 0))],
             6: [(scale_slots, (2, 0, 4))],
             11: [(widen_calib, ())],
         }
-        on_scalar = ((1, 0), (2, 0))
-        quantize_slot = {6: 1, 7: 2}
+        on_scalar = ((2, 0),)
+        quantize_slot = {7: 2}
         wide = CHUNKS.count(PART)
         units = [(c, g) for g in range(FG) for c in range(2)] + [(c, g) for c in range(2, wide) for g in range(FG)]
         tile_slot = [max(j + STAGE2_LAG, FIRST_TILE_SLOT + 3 * j // 5) for j in range(TILES)]
@@ -443,7 +443,7 @@ def tile_neural_mass_eeg_k5_kernel(
             whole = slot > FIRST_TILE_SLOT + 1 and units[slot - 1][1] == FG - 1 or slot in quantize_slot
             chunk = quantize_slot.get(slot, units[slot - 1][0])
             for j in tiles[:-1]:
-                stage2(j)
+                stage2(j, "turn" if j < 4 else "e_ps")
                 if whole:
                     quantize_p(chunk, 0)
                 calibrate(j)
@@ -455,9 +455,11 @@ def tile_neural_mass_eeg_k5_kernel(
             elif tile_slot[rounded] + ROUND_LAG < slot:
                 round_y(rounded)
                 rounded += 1
-            stage1(c, g, 1)
+            stage1(c, g, 1, *(("e_ps", 2) if 1 < slot < FIRST_TILE_SLOT - 1 else ()))
             for step, args in late_steps.get(slot, []):
                 step(*args)
+            if slot == len(units) - 1:
+                continue
             for j in tiles[-1:]:
                 stage2(j)
             if whole and len(tiles) < 2:
@@ -467,7 +469,7 @@ def tile_neural_mass_eeg_k5_kernel(
                 to_quantize = to_quantize[1:]
             for j in tiles[-1:]:
                 calibrate(j)
-            if rounded - turned >= 4:
+            if rounded - turned >= 4 and turned == 0:
                 for first in (turned, turned + 2):
                     turn_y(first, 2)
                     to_copy.append((first, 2))
@@ -476,40 +478,49 @@ def tile_neural_mass_eeg_k5_kernel(
                 round_y(rounded)
                 rounded += 1
 
-        stage1(7, 0, 0)
+        turn_y(4, 2)
+        turn_y(6, 2)
+        copy_turned(4, 2)
+        copy_turned(6, 2)
         scale_p(6, 1, 0)
+        stage2(10)
+        quantize_p(6, 0)
+        quantize_y(4, 4)
+        calibrate(10)
+        stage1(7, 0, 0)
+        for j in range(rounded, 10):
+            round_y(j)
         stage1(7, 1, 0)
         scale_p(7, 0, 0)
         stage2(11)
-        quantize_p(6, 0)
         calibrate(11)
-        round_y(10)
-        stage1(8, 0, 0)
         scale_p(7, 1, 0)
-        stage1(8, 1, 0)
+        stage1(8, 0, 0)
         scale_p(8, 0, 0)
-        quantize_p(7, 0)
+        stage1(8, 1, 0)
+        round_y(10)
         scale_p(8, 1, 0)
+        quantize_p(7, 0)
         stage2(12)
         quantize_p(8, 0)
         calibrate(12)
         round_y(11)
         stage2(13)
         spread_calib()
-        stage2(14, "u_ps", 3)
         turn_y(8, 2)
-        turn_y(10, 2)
         copy_turned(8, 2)
-        copy_turned(10, 2)
-        round_y(12)
+        stage2(14, "u_ps", 3)
         round_on_vector(13)
         calibrate(13)
         stage2(15, "u_ps", 3)
+        turn_y(10, 2)
+        round_y(12)
+        copy_turned(10, 2)
         round_on_vector(14)
         calibrate(14)
         round_on_vector(15)
         turn_y(12, 2)
-        turn_y(14, 1)
+        turn_y(14, 1, "e_ps", 2)
         turn_y(15, 1, "e_ps", 2)
         copy_turned(12, 2)
         copy_turned(14, 1)

@@ -39,6 +39,7 @@ TURN_LAG = 0
 QUANT_Y_LAG = 2
 FIRST_TILE_SLOT = 6
 VECTOR_TILES = (15,)
+ON_SCALAR = ((2, 0),)
 
 
 def starts(widths):
@@ -284,7 +285,11 @@ def tile_neural_mass_eeg_k5_kernel(
                     )
             if u == 0:
                 sig[c, g] = work.tile([P, PACK // per_bank, n, per_bank], F32, name="sig", tag="sig", bufs=6, align_bytes=64)
-            nc.scalar.activation(out=sig[c, g][:, u], in_=u_ps[:].rearrange("p e n -> p n e"), func=ACT.Sigmoid)
+            if (c, g) in ON_SCALAR:
+                by_slot = sig[c, g][:].rearrange("p u n e -> p (u n e)").rearrange("p (t n) -> p t n", t=PACK)
+                nc.scalar.activation(out=by_slot[:, u * per_bank : (u + 1) * per_bank], in_=u_ps[:], func=ACT.Sigmoid)
+            else:
+                nc.scalar.activation(out=sig[c, g][:, u], in_=u_ps[:].rearrange("p e n -> p n e"), func=ACT.Sigmoid)
 
         def scale_p(c, g, h):
             n = CHUNKS[c]
@@ -304,14 +309,15 @@ def tile_neural_mass_eeg_k5_kernel(
             nc.scalar.copy(out=gain_sb[:], in_=gain_ps[:, : FG * PACK])
 
         def scale_slots(c, t0, t1):
+            by_slot = sig[c, 0][:].rearrange("p u n e -> p (u n e)").rearrange("p (t n) -> p t n", t=PACK)
             if t0 == 0:
-                p_slot[c] = work.tile([P, PACK, PART], BF16, name="p_slot", tag="p_slot", bufs=1, align_bytes=64)
+                p_slot[c] = work.tile([P, PACK, CHUNKS[c]], BF16, name="p_slot", tag="p_slot", bufs=1, align_bytes=64)
             for t in range(t0, t1):
-                nc.scalar.activation(out=p_slot[c][:, t, :], in_=sig[c, 0][:, t // 2, :, t % 2], func=ACT.Copy, scale=gain_sb[:, t : t + 1])
+                nc.scalar.activation(out=p_slot[c][:, t, :], in_=by_slot[:, t, :], func=ACT.Copy, scale=gain_sb[:, t : t + 1])
 
         def interleave_p(c, n0, n1):
             if (c, 0) not in p_bf:
-                p_bf[c, 0] = work.tile([P, FG, PART, PACK], BF16, name="p_bf", tag="p_bf", bufs=4, align_bytes=64)
+                p_bf[c, 0] = work.tile([P, FG, CHUNKS[c], PACK], BF16, name="p_bf", tag="p_bf", bufs=4, align_bytes=64)
             nc.scalar.copy(
                 out=p_bf[c, 0][:, 0, n0:n1].rearrange("p (m i) t -> p m t i", i=RUN),
                 in_=p_slot[c][:, :, n0:n1].rearrange("p t (m i) -> p m t i", i=RUN),
@@ -422,11 +428,10 @@ def tile_neural_mass_eeg_k5_kernel(
             6: [(scale_slots, (2, 0, 4))],
             11: [(widen_calib, ())],
         }
-        on_scalar = ((2, 0),)
         quantize_slot = {7: 2}
         wide = CHUNKS.count(PART)
         units = [(c, g) for g in range(FG) for c in range(2)] + [(c, g) for c in range(2, wide) for g in range(FG)]
-        tile_slot = [max(j + STAGE2_LAG, FIRST_TILE_SLOT + 3 * j // 5) for j in range(TILES)]
+        tile_slot = [max(j + STAGE2_LAG, FIRST_TILE_SLOT + 2 * j // 3) for j in range(TILES)]
         to_copy = []
         to_quantize = []
         rounded = 0
@@ -436,7 +441,7 @@ def tile_neural_mass_eeg_k5_kernel(
             stage1(c, g, 0)
             for step, args in before_gain.get(slot, []):
                 step(*args)
-            if slot > 0 and units[slot - 1] not in on_scalar:
+            if slot > 0 and units[slot - 1] not in ON_SCALAR:
                 scale_p(*units[slot - 1], 0)
             for step, args in lead_steps.get(slot, []):
                 step(*args)
@@ -452,7 +457,7 @@ def tile_neural_mass_eeg_k5_kernel(
                     copy_turned(*pair)
                 to_quantize.append((turned - 4, 4))
                 to_copy = []
-            elif tile_slot[rounded] + ROUND_LAG < slot:
+            elif tile_slot[rounded] + ROUND_LAG < slot < len(units) - 1:
                 round_y(rounded)
                 rounded += 1
             stage1(c, g, 1, *(("e_ps", 2) if 1 < slot < FIRST_TILE_SLOT - 1 else ()))
@@ -474,7 +479,7 @@ def tile_neural_mass_eeg_k5_kernel(
                     turn_y(first, 2)
                     to_copy.append((first, 2))
                 turned += 4
-            if tile_slot[rounded] + ROUND_LAG <= slot:
+            if tile_slot[rounded] + ROUND_LAG <= slot and slot < len(units) - 2:
                 round_y(rounded)
                 rounded += 1
 
@@ -497,15 +502,15 @@ def tile_neural_mass_eeg_k5_kernel(
         scale_p(7, 1, 0)
         stage1(8, 0, 0)
         scale_p(8, 0, 0)
+        stage2(12)
+        quantize_p(7, 0)
+        calibrate(12)
         stage1(8, 1, 0)
         round_y(10)
         scale_p(8, 1, 0)
-        quantize_p(7, 0)
-        stage2(12)
-        quantize_p(8, 0)
-        calibrate(12)
-        round_y(11)
         stage2(13)
+        quantize_p(8, 0)
+        round_y(11)
         spread_calib()
         turn_y(8, 2)
         copy_turned(8, 2)

@@ -27,18 +27,18 @@ RUN = 4
 TILES = T // P
 CHUNKS = [256] * 7 + [128] * 2
 RATE_LOADS = [256, 256, 512, 1024]
-BG_LOADS = [512, 512, 1024]
+BG_LOADS = [512, 512, 768, 256]
 CODE_STORES = [512, 1024, 1536, 2048]
 SCALE_STORES = [1024, 2048]
 TURN_RUNS = [4, 4, 4, 2, 1, 1]
-WARM_PASSES = 10
+WARM_PASSES = 11
 WARM_N = 256
 STAGE2_LAG = 3
 ROUND_LAG = 1
 TURN_LAG = 0
 QUANT_Y_LAG = 2
 FIRST_TILE_SLOT = 6
-VECTOR_TILES = (15,)
+SPLIT_TILES = (14, 15)
 ON_SCALAR = ((2, 0),)
 
 
@@ -83,11 +83,11 @@ def tile_neural_mass_eeg_k5_kernel(
         lead_sc = [placed(keep, "lead_sc%d" % g, [P, 1, S], 192)[:, 0, :] for g in range(FG)]
         bg = [kept("bg%d" % i, [P, w // P, S], BF16) for i, w in enumerate(BG_LOADS)]
         calib_all = kept("calib_all", [P, S], BF16)
-        calib_col = kept("calib_col", [P, PACK], BF16)
-        calib_f32 = kept("calib_f32", [P, PACK], F32)
         gain_row = kept("gain_row", [FG, K_PASS], BF16)
         gain_sq = kept("gain_sq", [P, PACK, P], F32)
         gain_ps = psum.tile([P, BANK], F32, name="gain_ps", tag="gain_ps", bufs=1)
+        calib_col = kept("calib_col", [P, PACK], BF16)
+        calib_f32 = kept("calib_f32", [P, PACK], F32)
         gain_sb = kept("gain_sb", [P, FG * PACK], F32)
         zero_bf = kept("zero_bf", [P, PACK * WARM_N], BF16)
         zero_w = kept("zero_w", [P, PACK * WARM_N], U8)
@@ -228,9 +228,9 @@ def tile_neural_mass_eeg_k5_kernel(
         nc.vector.quantize_mx(out=zero_w[:].bitcast(FP8X4), scales=zero_sc[:], in_=zero_bf[:])
         nc.scalar.activation(out=warm[:], in_=warm[:], func=ACT.Sigmoid)
         order_gain()
-        warm_up(WARM_PASSES - 5)
+        warm_up(WARM_PASSES - 4)
         turn_gain()
-        warm_up(5)
+        warm_up(4)
         permute_conn_words(0, 0, 2)
         permute_conn_words(0, 2, 4)
         permute_conn_scales(0, 0, 2)
@@ -247,12 +247,15 @@ def tile_neural_mass_eeg_k5_kernel(
             load_rate_scales(1, q, nc.sync)
         load_bg(0)
         nc.sync.dma_start(out=calib_all[:], in_=calib.partition_broadcast(P))
+        load_bg(3)
         load_rate_words(3)
         load_bg(1)
         load_bg(2)
         nc.sync.dma_start(out=calib_col[:], in_=calib.rearrange("(p t) -> p t", t=PACK))
 
         chunk_t0 = starts(CHUNKS)
+        spare = lead_il[1][:].rearrange("p s t -> p (s t)").bitcast(F32).rearrange("p (a t m) -> p a t m", a=2, t=PACK)
+        bg_scaled = {14: spare[:, 0], 15: spare[:, 1]}
         calib_ps = {}
         sig = {}
         p_bf = {}
@@ -348,21 +351,52 @@ def tile_neural_mass_eeg_k5_kernel(
                     stop=(g == FG - 1),
                 )
             i, off = locate(BG_LOADS, P * j)
-            tsum[j] = work.tile([P, S], F32, name="tsum", tag="tsum", bufs=4)
-            nc.vector.tensor_tensor(out=tsum[j][:], in0=bg[i][:, off // P, :], in1=e_ps[:], op=ALU.add)
-
-        def calibrate(j):
-            y[j] = work.tile([P, S], F32, name="y", tag="y", bufs=6)
-            if j in VECTOR_TILES:
+            tsum[j] = work.tile([P, S], F32, name="tsum", tag="tsum", bufs=12)
+            if j in SPLIT_TILES:
                 nc.vector.tensor_tensor(
-                    out=y[j][:].rearrange("p (m t) -> p m t", t=PACK),
-                    in0=tsum[j][:].rearrange("p (m t) -> p m t", t=PACK),
-                    in1=calib_ps["tile"][:].rearrange("p t m -> p m t"),
+                    out=tsum[j][:].rearrange("p (t m) -> p t m", t=PACK),
+                    in0=calib_all[:].rearrange("p (m t) -> p t m", t=PACK),
+                    in1=e_ps[:].rearrange("p (m t) -> p t m", t=PACK),
                     op=ALU.mult,
                 )
             else:
-                nc.gpsimd.tensor_tensor(out=y[j][:], in0=tsum[j][:], in1=calib_all[:], op=ALU.mult)
+                nc.vector.tensor_tensor(out=tsum[j][:], in0=bg[i][:, off // P, :], in1=e_ps[:], op=ALU.add)
+
+        def calibrate(j):
+            y[j] = work.tile([P, S], F32, name="y", tag="y", bufs=6)
+            nc.gpsimd.tensor_tensor(out=y[j][:], in0=tsum[j][:], in1=calib_all[:], op=ALU.mult)
             nc.sync.dma_start(out=out_0[P * j : P * (j + 1), :], in_=y[j][:])
+
+        def scale_bg(j):
+            i, off = locate(BG_LOADS, P * j)
+            nc.gpsimd.tensor_tensor(
+                out=bg_scaled[j],
+                in0=bg[i][:, off // P, :].rearrange("p (m t) -> p t m", t=PACK),
+                in1=calib_all[:].rearrange("p (m t) -> p t m", t=PACK),
+                op=ALU.mult,
+            )
+
+        def add_scaled(j):
+            y[j] = work.tile([P, S], F32, name="y", tag="y", bufs=6)
+            nc.vector.tensor_tensor(
+                out=y[j][:].rearrange("p (m i t) -> p m t i", i=RUN, t=PACK),
+                in0=tsum[j][:].rearrange("p (t m i) -> p m t i", t=PACK, i=RUN),
+                in1=bg_scaled[j].rearrange("p t (m i) -> p m t i", i=RUN),
+                op=ALU.add,
+            )
+            nc.sync.dma_start(out=out_0[P * j : P * (j + 1), :], in_=y[j][:])
+
+        def turn_terms(j):
+            yt_ps[j] = psum.tile([P, PACK, P], F32, name="yt_ps", tag="e_ps", bufs=2)
+            for t in range(PACK):
+                nc.tensor.matmul(yt_ps[j][:, t, :], bg_scaled[j][:, t, :], ident[:], start=True, stop=False, is_transpose=True)
+                nc.tensor.matmul(yt_ps[j][:, t, :], tsum[j][:, P * t : P * (t + 1)], ident[:], start=False, stop=True, is_transpose=True)
+
+        def round_turned(j):
+            nc.scalar.copy(
+                out=yt[:, PACK * P * j : PACK * P * (j + 1)].rearrange("p (m t) -> p m t", t=PACK),
+                in_=yt_ps[j][:].rearrange("p t m -> p m t"),
+            )
 
         def widen_calib():
             nc.gpsimd.tensor_copy(out=calib_f32[:], in_=calib_col[:])
@@ -424,9 +458,10 @@ def tile_neural_mass_eeg_k5_kernel(
             1: [(interleave_lead, (0, "gpsimd", 0, 3 * S // 4))],
             2: [(interleave_lead, (0, "scalar", 3 * S // 4, S)), (interleave_lead, (1, "vector", 0, S // 2))],
             3: [(interleave_lead, (1, "scalar", S // 2, 3 * S // 4)), (quantize_lead, (0,)), (quantize_p, (0, 0))],
-            4: [(interleave_lead, (1, "scalar", 3 * S // 4, S)), (quantize_lead, (1,)), (quantize_p, (1, 0))],
+            4: [(interleave_lead, (1, "scalar", 3 * S // 4, S)), (quantize_lead, (1,)), (quantize_p, (1, 0)), (scale_bg, (15,))],
             6: [(scale_slots, (2, 0, 4))],
             11: [(widen_calib, ())],
+            13: [(scale_bg, (14,))],
         }
         quantize_slot = {7: 2}
         wide = CHUNKS.count(PART)
@@ -517,20 +552,18 @@ def tile_neural_mass_eeg_k5_kernel(
         stage2(14, "u_ps", 3)
         round_on_vector(13)
         calibrate(13)
-        stage2(15, "u_ps", 3)
         turn_y(10, 2)
+        stage2(15, "u_ps", 3)
         round_y(12)
         copy_turned(10, 2)
-        round_on_vector(14)
-        calibrate(14)
-        round_on_vector(15)
+        turn_terms(14)
         turn_y(12, 2)
-        turn_y(14, 1, "e_ps", 2)
-        turn_y(15, 1, "e_ps", 2)
+        turn_terms(15)
+        round_turned(14)
         copy_turned(12, 2)
-        copy_turned(14, 1)
-        copy_turned(15, 1)
-        calibrate(15)
+        round_turned(15)
+        add_scaled(14)
+        add_scaled(15)
         quantize_y(8, 4)
         quantize_y(12, 3)
         quantize_y(15, 1)

@@ -31,8 +31,6 @@ BG_LOADS = [512, 512, 768, 256]
 CODE_STORES = [512, 1024, 1536, 2048]
 SCALE_STORES = [1024, 2048]
 TURN_RUNS = [4, 4, 4, 2, 1, 1]
-WARM_PASSES = 11
-WARM_N = 256
 STAGE2_LAG = 3
 ROUND_LAG = 1
 TURN_LAG = 0
@@ -89,11 +87,7 @@ def tile_neural_mass_eeg_k5_kernel(
         calib_col = kept("calib_col", [P, PACK], BF16)
         calib_f32 = kept("calib_f32", [P, PACK], F32)
         gain_sb = kept("gain_sb", [P, FG * PACK], F32)
-        zero_bf = kept("zero_bf", [P, PACK * WARM_N], BF16)
-        zero_w = kept("zero_w", [P, PACK * WARM_N], U8)
-        zero_sc = kept("zero_sc", [P, WARM_N], U8)
         ident = kept("ident", [P, P], F32)
-        warm = kept("warm", [P, 1], F32)
         y_w = kept("y_w", [P, PACK * T], U8)
         yt = kept("yt", [P, PACK * T], BF16)
         y_sc = kept("y_sc", [P, T], U8)
@@ -192,20 +186,6 @@ def tile_neural_mass_eeg_k5_kernel(
                 in_=gain_row[:].rearrange("g (q t r) -> g t q r", t=PACK, r=4),
             )
 
-        warm_ps = psum.tile([P, WARM_N], F32, name="warm_ps", tag="e_ps", bufs=2)
-
-        def warm_up(passes):
-            for i in range(passes):
-                nc.tensor.matmul_mx(
-                    out=warm_ps[:],
-                    lhsT=zero_w[:, : PACK * P].bitcast(FP8X4),
-                    lhsT_scale=zero_sc[:, :P],
-                    rhs=zero_w[:].bitcast(FP8X4),
-                    rhs_scale=zero_sc[:],
-                    start=True,
-                    stop=True,
-                )
-
         load_gain()
         load_rate_words(0)
         load_conn_words(0)
@@ -222,15 +202,9 @@ def tile_neural_mass_eeg_k5_kernel(
         load_rate_words(1)
         load_conn_words(1)
         make_identity(nc, ident[:])
-        nc.vector.memset(zero_bf[:], 0.0)
-        nc.vector.memset(warm[:], 0.0)
         nc.vector.memset(gain_sq[:], 0.0)
-        nc.vector.quantize_mx(out=zero_w[:].bitcast(FP8X4), scales=zero_sc[:], in_=zero_bf[:])
-        nc.scalar.activation(out=warm[:], in_=warm[:], func=ACT.Sigmoid)
         order_gain()
-        warm_up(WARM_PASSES - 4)
         turn_gain()
-        warm_up(4)
         permute_conn_words(0, 0, 2)
         permute_conn_words(0, 2, 4)
         permute_conn_scales(0, 0, 2)

from contextlib import ExitStack

import concourse.mybir as mybir
from concourse.masks import make_identity

T, K, F, S = 2048, 1536, 1024, 512
FLOPS = 2 * T * K * F + 2 * T * F * S

F32 = mybir.dt.float32
BF16 = mybir.dt.bfloat16
I32 = mybir.dt.int32
U8 = mybir.dt.uint8
FP4X4 = mybir.dt.float4_e2m1fn_x4
FP8X4 = mybir.dt.float8_e4m3fn_x4
ACT = mybir.ActivationFunctionType
ALU = mybir.AluOpType

P = 128
PACK = 4
K_PASS = P * PACK
KP = K // K_PASS
FG = F // K_PASS
BANK = 512
PART = 256
SPAN = 256
RUN = 4
TILES = T // P
CHUNKS = [256] * 7 + [128] * 2
RATE_LOADS = [256, 256, 512, 1024]
BG_LOADS = [512, 512, 768, 256]
CODE_STORES = [512, 1024, 1536, 2048]
SCALE_STORES = [1024, 2048]
TURN_RUNS = [4, 4, 4, 2, 1, 1]
STAGE2_LAG = 3
ROUND_LAG = 1
TURN_LAG = 0
QUANT_Y_LAG = 2
FIRST_TILE_SLOT = 6
SPLIT_TILES = (14, 15)
ON_SCALAR = ((2, 0),)


def starts(widths):
    return [sum(widths[:i]) for i in range(len(widths))]


def locate(widths, t0):
    first = starts(widths)
    i = max(j for j in range(len(widths)) if first[j] <= t0)
    return i, t0 - first[i]


def tile_neural_mass_eeg_k5_kernel(
    tc, rate_words, rate_scales, conn_words, conn_scales, gain, lead, background, calib, out_0, out_1, out_2
):
    nc = tc.nc
    with ExitStack() as ctx:
        keep = ctx.enter_context(tc.tile_pool(name="keep", bufs=1))
        work = ctx.enter_context(tc.tile_pool(name="work", bufs=3))
        psum = ctx.enter_context(tc.psum_pool(name="psum", bufs=2))
        ctx.enter_context(tc.manual_schedule())

        def kept(name, shape, dtype):
            return keep.tile(shape, dtype, name=name, align_bytes=64)

        def placed(pool, name, shape, start, **kw):
            size = shape[1] * shape[2]
            tile = pool.tile([P, size + SPAN], U8, name=name, align_bytes=SPAN, **kw)
            return tile[:, start : start + size].rearrange("p (a b) -> p a b", a=shape[1])

        rate_scale_loads = [768, T - 768]
        conn_raw = [kept("conn_raw%d" % g, [P, KP, 2 * K_PASS], U8) for g in range(FG)]
        conn_sc_raw = kept("conn_sc_raw", [P, KP, F], U8)
        conn_w = [placed(keep, "conn_w%d" % g, [P, PACK, KP * 2 * P], 0).rearrange("p t (k c) -> p t k c", k=KP) for g in range(FG)]
        conn_sc = [placed(keep, "conn_sc%d" % g, [P, PACK, KP * P], 64).rearrange("p t (k c) -> p t k c", k=KP) for g in range(FG)]
        rate_w = [placed(keep, "rate_w%d" % i, [P, KP, 2 * w], 128) for i, w in enumerate(RATE_LOADS)]
        rate_sc = [placed(keep, "rate_sc%d" % i, [P, KP, w], 192) for i, w in enumerate(rate_scale_loads)]
        lead_raw = [kept("lead_raw%d" % g, [P, PACK, S], BF16) for g in range(FG)]
        lead_il = [kept("lead_il%d" % g, [P, S, PACK], BF16) for g in range(FG)]
        lead_w = [placed(keep, "lead_w%d" % g, [P, 1, PACK * S], 128)[:, 0, :] for g in range(FG)]
        lead_sc = [placed(keep, "lead_sc%d" % g, [P, 1, S], 192)[:, 0, :] for g in range(FG)]
        bg = [kept("bg%d" % i, [P, w // P, S], BF16) for i, w in enumerate(BG_LOADS)]
        calib_all = kept("calib_all", [P, S], BF16)
        gain_row = kept("gain_row", [FG, K_PASS], BF16)
        gain_sq = kept("gain_sq", [P, PACK, P], F32)
        gain_ps = psum.tile([P, BANK], F32, name="gain_ps", tag="gain_ps", bufs=1)
        calib_col = kept("calib_col", [P, PACK], BF16)
        calib_f32 = kept("calib_f32", [P, PACK], F32)
        gain_sb = kept("gain_sb", [P, FG * PACK], F32)
        ident = kept("ident", [P, P], F32)
        y_w = kept("y_w", [P, PACK * T], U8)
        yt = kept("yt", [P, PACK * T], BF16)
        y_sc = kept("y_sc", [P, T], U8)

        rate_words32 = rate_words.bitcast(I32)
        conn_words32 = conn_words.bitcast(I32)
        rate_scales32 = rate_scales.bitcast(I32)
        conn_scales32 = conn_scales.bitcast(I32)

        def zero(tile):
            nc.vector.memset(tile[:].rearrange("p k c -> p (k c)").bitcast(I32), 0)

        def load_conn_words(g):
            nc.sync.dma_start(
                out=conn_raw[g][:].bitcast(I32),
                in_=conn_words32[:, :, 256 * g : 256 * (g + 1)].rearrange("k p c -> p k c"),
            )

        def load_rate_words(c):
            t0 = starts(RATE_LOADS)[c]
            nc.sync.dma_start(
                out=rate_w[c][:].bitcast(I32),
                in_=rate_words32[:, :, t0 // 2 : (t0 + RATE_LOADS[c]) // 2].rearrange("k p c -> p k c"),
            )

        def load_rate_scales(i, q, queue):
            t0 = starts(rate_scale_loads)[i]
            queue.dma_start(
                out=rate_sc[i][q:P:32].bitcast(I32),
                in_=rate_scales32[:, q:16:4, t0 // 4 : (t0 + rate_scale_loads[i]) // 4].rearrange(
                    "k r c -> r k c"
                ),
            )

        def load_conn_scales(q, queue):
            queue.dma_start(
                out=conn_sc_raw[q:P:32].bitcast(I32),
                in_=conn_scales32[:, q:16:4, :].rearrange("k r c -> r k c"),
            )

        def load_lead(g):
            rows = lead[K_PASS * g : K_PASS * (g + 1), :].rearrange("(q t r) s -> r q t s", t=PACK, r=4)
            for r in range(4):
                nc.sync.dma_start(out=lead_raw[g][r:P:4], in_=rows[r])

        def load_gain():
            nc.scalar.dma_start(out=gain_row[:], in_=gain.rearrange("(g f) -> g f", g=FG))

        def load_bg(i):
            t0 = starts(BG_LOADS)[i]
            nc.sync.dma_start(out=bg[i][:], in_=background[t0 : t0 + BG_LOADS[i], :].rearrange("(a p) s -> p a s", p=P))

        def permute_conn_words(g, t0, t1):
            n = t1 - t0
            nc.vector.tensor_copy(
                out=conn_w[g][:, t0:t1].rearrange("p t k c -> p (t k c)").bitcast(I32).rearrange("p (t m w) -> p t m w", t=n, w=2),
                in_=conn_raw[g][:].rearrange("p k c -> p (k c)").bitcast(I32).rearrange("p (m t w) -> p t m w", t=PACK, w=2)[:, t0:t1],
            )

        def permute_conn_scales(g, t0, t1):
            n = t1 - t0
            nc.vector.tensor_copy(
                out=conn_sc[g][:, t0:t1].rearrange("p t k c -> p (t k c)").bitcast(I32).rearrange("p (t k m) -> p t k m", t=n, k=KP),
                in_=conn_sc_raw[:].bitcast(I32)[:, :, P * g : P * (g + 1)].rearrange("p k (m t) -> p t k m", t=PACK)[:, t0:t1],
            )

        def interleave_lead(g, engine, s0, s1):
            if engine == "gpsimd":
                nc.gpsimd.tensor_scalar(
                    out=lead_il[g][:, s0:s1, :],
                    in0=lead_raw[g][:, :, s0:s1].rearrange("p t s -> p s t"),
                    scalar1=1.0,
                    scalar2=0.0,
                    op0=ALU.mult,
                    op1=ALU.add,
                )
            else:
                copy = nc.vector.tensor_copy if engine == "vector" else nc.scalar.copy
                copy(
                    out=lead_il[g][:, s0:s1, :].rearrange("p (c i) t -> p c t i", i=4),
                    in_=lead_raw[g][:, :, s0:s1].rearrange("p t (c i) -> p c t i", i=4),
                )

        def quantize_lead(g):
            nc.vector.quantize_mx(
                out=lead_w[g][:].bitcast(FP8X4), scales=lead_sc[g][:], in_=lead_il[g][:].rearrange("p s t -> p (s t)")
            )

        def turn_gain():
            for t in range(PACK):
                nc.tensor.transpose(gain_ps[:, t:BANK:PACK], gain_sq[:, t, :], ident[:])

        def order_gain():
            nc.vector.tensor_copy(
                out=gain_sq[:FG].rearrange("g t (q r) -> g t q r", r=4),
                in_=gain_row[:].rearrange("g (q t r) -> g t q r", t=PACK, r=4),
            )

        load_gain()
        load_rate_words(0)
        load_conn_words(0)
        zero(conn_sc_raw)
        zero(rate_sc[0])
        load_conn_scales(0, nc.scalar)
        load_conn_scales(1, nc.sync)
        load_conn_scales(2, nc.scalar)
        load_conn_scales(3, nc.sync)
        load_rate_scales(0, 0, nc.gpsimd)
        load_rate_scales(0, 1, nc.scalar)
        load_rate_scales(0, 2, nc.sync)
        load_rate_scales(0, 3, nc.sync)
        load_rate_words(1)
        load_conn_words(1)
        make_identity(nc, ident[:])
        nc.vector.memset(gain_sq[:], 0.0)
        order_gain()
        turn_gain()
        permute_conn_words(0, 0, 2)
        permute_conn_words(0, 2, 4)
        permute_conn_scales(0, 0, 2)
        permute_conn_scales(0, 2, 4)
        zero(rate_sc[1])
        permute_conn_scales(1, 0, 4)
        permute_conn_words(1, 0, 2)
        permute_conn_words(1, 2, 4)

        load_lead(0)
        load_lead(1)
        load_rate_words(2)
        for q in range(4):
            load_rate_scales(1, q, nc.sync)
        load_bg(0)
        nc.sync.dma_start(out=calib_all[:], in_=calib.partition_broadcast(P))
        load_bg(3)
        load_rate_words(3)
        load_bg(1)
        load_bg(2)
        nc.sync.dma_start(out=calib_col[:], in_=calib.rearrange("(p t) -> p t", t=PACK))

        chunk_t0 = starts(CHUNKS)
        spare = lead_il[1][:].rearrange("p s t -> p (s t)").bitcast(F32).rearrange("p (a t m) -> p a t m", a=2, t=PACK)
        bg_scaled = {14: spare[:, 0], 15: spare[:, 1]}
        calib_ps = {}
        sig = {}
        p_bf = {}
        p_slot = {}
        p_w = {}
        p_sc = {}
        e_ps = {}
        tsum = {}
        y = {}
        y_bf = {}
        yt_ps = {}

        def stage1(c, g, u, tag="u_ps", bufs=3):
            n = CHUNKS[c]
            per_bank = BANK // n
            i, off = locate(RATE_LOADS, chunk_t0[c])
            j, soff = locate(rate_scale_loads, chunk_t0[c])
            u_ps = psum.tile([P, per_bank, n], F32, name="u_ps", tag=tag, bufs=bufs)
            for e in range(per_bank):
                t = u * per_bank + e
                for k in range(KP):
                    nc.tensor.matmul_mx(
                        out=u_ps[:, e, :],
                        lhsT=conn_w[g][:, t, k, :].bitcast(FP4X4),
                        lhsT_scale=conn_sc[g][:, t, k, :],
                        rhs=rate_w[i][:, k, 2 * off : 2 * (off + n)].bitcast(FP4X4),
                        rhs_scale=rate_sc[j][:, k, soff : soff + n],
                        start=(k == 0),
                        stop=(k == KP - 1),
                    )
            if u == 0:
                sig[c, g] = work.tile([P, PACK // per_bank, n, per_bank], F32, name="sig", tag="sig", bufs=6, align_bytes=64)
            if (c, g) in ON_SCALAR:
                by_slot = sig[c, g][:].rearrange("p u n e -> p (u n e)").rearrange("p (t n) -> p t n", t=PACK)
                nc.scalar.activation(out=by_slot[:, u * per_bank : (u + 1) * per_bank], in_=u_ps[:], func=ACT.Sigmoid)
            else:
                nc.scalar.activation(out=sig[c, g][:, u], in_=u_ps[:].rearrange("p e n -> p n e"), func=ACT.Sigmoid)

        def scale_p(c, g, h):
            n = CHUNKS[c]
            w = min(n, PART)
            if (c, h) not in p_bf:
                p_bf[c, h] = work.tile([P, FG, w, PACK], BF16, name="p_bf", tag="p_bf", bufs=4, align_bytes=64)
            per_bank = BANK // n
            gains = gain_ps[:, PACK * g : PACK * (g + 1)].rearrange("p (u e) -> p u e", e=per_bank)
            nc.vector.tensor_tensor(
                out=p_bf[c, h][:, g].rearrange("p n (u e) -> p n u e", e=per_bank),
                in0=sig[c, g][:].rearrange("p u n e -> p n u e"),
                in1=gains.unsqueeze(1).to_broadcast([P, w, PACK // per_bank, per_bank]),
                op=ALU.mult,
            )

        def copy_gains():
            nc.scalar.copy(out=gain_sb[:], in_=gain_ps[:, : FG * PACK])

        def scale_slots(c, t0, t1):
            by_slot = sig[c, 0][:].rearrange("p u n e -> p (u n e)").rearrange("p (t n) -> p t n", t=PACK)
            if t0 == 0:
                p_slot[c] = work.tile([P, PACK, CHUNKS[c]], BF16, name="p_slot", tag="p_slot", bufs=1, align_bytes=64)
            for t in range(t0, t1):
                nc.scalar.activation(out=p_slot[c][:, t, :], in_=by_slot[:, t, :], func=ACT.Copy, scale=gain_sb[:, t : t + 1])

        def interleave_p(c, n0, n1):
            if (c, 0) not in p_bf:
                p_bf[c, 0] = work.tile([P, FG, CHUNKS[c], PACK], BF16, name="p_bf", tag="p_bf", bufs=4, align_bytes=64)
            nc.scalar.copy(
                out=p_bf[c, 0][:, 0, n0:n1].rearrange("p (m i) t -> p m t i", i=RUN),
                in_=p_slot[c][:, :, n0:n1].rearrange("p t (m i) -> p m t i", i=RUN),
            )

        def quantize_p(c, h):
            w = min(CHUNKS[c], PART)
            p_w[c, h] = placed(work, "p_w", [P, FG, PACK * w], 0, tag="p_w", bufs=4)
            p_sc[c, h] = placed(work, "p_sc", [P, FG, w], 64, tag="p_sc", bufs=4)
            nc.vector.quantize_mx(
                out=p_w[c, h][:].rearrange("p g w -> p (g w)").bitcast(FP8X4),
                scales=p_sc[c, h][:].rearrange("p g n -> p (g n)"),
                in_=p_bf[c, h][:].rearrange("p g n t -> p (g n t)"),
            )

        def stage2(j, tag="e_ps", bufs=2):
            c, off = locate(CHUNKS, P * j)
            h, a = divmod(off // P, PART // P)
            e_ps = psum.tile([P, S], F32, name="e_ps", tag=tag, bufs=bufs)
            for g in range(FG):
                nc.tensor.matmul_mx(
                    out=e_ps[:],
                    lhsT=p_w[c, h][:, g, PACK * P * a : PACK * P * (a + 1)].bitcast(FP8X4),
                    lhsT_scale=p_sc[c, h][:, g, P * a : P * (a + 1)],
                    rhs=lead_w[g][:].bitcast(FP8X4),
                    rhs_scale=lead_sc[g][:],
                    start=(g == 0),
                    stop=(g == FG - 1),
                )
            i, off = locate(BG_LOADS, P * j)
            tsum[j] = work.tile([P, S], F32, name="tsum", tag="tsum", bufs=12)
            if j in SPLIT_TILES:
                nc.vector.tensor_tensor(
                    out=tsum[j][:].rearrange("p (t m) -> p t m", t=PACK),
                    in0=calib_all[:].rearrange("p (m t) -> p t m", t=PACK),
                    in1=e_ps[:].rearrange("p (m t) -> p t m", t=PACK),
                    op=ALU.mult,
                )
            else:
                nc.vector.tensor_tensor(out=tsum[j][:], in0=bg[i][:, off // P, :], in1=e_ps[:], op=ALU.add)

        def calibrate(j):
            y[j] = work.tile([P, S], F32, name="y", tag="y", bufs=6)
            nc.gpsimd.tensor_tensor(out=y[j][:], in0=tsum[j][:], in1=calib_all[:], op=ALU.mult)
            nc.sync.dma_start(out=out_0[P * j : P * (j + 1), :], in_=y[j][:])

        def scale_bg(j):
            i, off = locate(BG_LOADS, P * j)
            nc.gpsimd.tensor_tensor(
                out=bg_scaled[j],
                in0=bg[i][:, off // P, :].rearrange("p (m t) -> p t m", t=PACK),
                in1=calib_all[:].rearrange("p (m t) -> p t m", t=PACK),
                op=ALU.mult,
            )

        def add_scaled(j):
            y[j] = work.tile([P, S], F32, name="y", tag="y", bufs=6)
            nc.vector.tensor_tensor(
                out=y[j][:].rearrange("p (m i t) -> p m t i", i=RUN, t=PACK),
                in0=tsum[j][:].rearrange("p (t m i) -> p m t i", t=PACK, i=RUN),
                in1=bg_scaled[j].rearrange("p t (m i) -> p m t i", i=RUN),
                op=ALU.add,
            )
            nc.sync.dma_start(out=out_0[P * j : P * (j + 1), :], in_=y[j][:])

        def turn_terms(j):
            yt_ps[j] = psum.tile([P, PACK, P], F32, name="yt_ps", tag="e_ps", bufs=2)
            for t in range(PACK):
                nc.tensor.matmul(yt_ps[j][:, t, :], bg_scaled[j][:, t, :], ident[:], start=True, stop=False, is_transpose=True)
                nc.tensor.matmul(yt_ps[j][:, t, :], tsum[j][:, P * t : P * (t + 1)], ident[:], start=False, stop=True, is_transpose=True)

        def round_turned(j):
            nc.scalar.copy(
                out=yt[:, PACK * P * j : PACK * P * (j + 1)].rearrange("p (m t) -> p m t", t=PACK),
                in_=yt_ps[j][:].rearrange("p t m -> p m t"),
            )

        def widen_calib():
            nc.gpsimd.tensor_copy(out=calib_f32[:], in_=calib_col[:])

        def spread_calib():
            calib_ps["tile"] = psum.tile([P, PACK, P], F32, name="calib_ps", tag="u_ps", bufs=3)
            for t in range(PACK):
                nc.tensor.transpose(calib_ps["tile"][:, t, :], calib_f32[:, t : t + 1].to_broadcast([P, P]), ident[:])

        def round_on_vector(j):
            y_bf[j] = work.tile([P, 2, P, 2], BF16, name="y_bf", tag="y_bf", bufs=8)
            nc.vector.tensor_tensor(
                out=y_bf[j][:],
                in0=tsum[j][:].rearrange("p (m u e) -> p u m e", u=2, e=2),
                in1=calib_ps["tile"][:].rearrange("p (u e) m -> p u m e", u=2),
                op=ALU.mult,
            )

        def round_y(j):
            y_bf[j] = work.tile([P, 2, P, 2], BF16, name="y_bf", tag="y_bf", bufs=8)
            nc.scalar.copy(out=y_bf[j][:], in_=y[j][:].rearrange("p (m u e) -> p u m e", u=2, e=2))

        def turn_y(j0, tiles, tag="turn", bufs=2):
            yt_ps[j0] = psum.tile([P, tiles, 2, P], F32, name="yt_ps", tag=tag, bufs=bufs)
            for a in range(tiles):
                words = y_bf[j0 + a][:].rearrange("p u m e -> p (u m e)").bitcast(F32)
                for u in range(2):
                    nc.tensor.transpose(yt_ps[j0][:, a, u, :], words[:, P * u : P * (u + 1)], ident[:])

        def copy_turned(j0, tiles, engine=nc.scalar.copy):
            engine(
                out=yt[:, PACK * P * j0 : PACK * P * (j0 + tiles)].bitcast(F32).rearrange("p (a m u) -> p a m u", m=P, u=2),
                in_=yt_ps[j0][:].rearrange("p a u m -> p a m u"),
            )

        def quantize_y(j0, tiles):
            t0, t1 = P * j0, P * (j0 + tiles)
            nc.vector.quantize_mx(out=y_w[:, PACK * t0 : PACK * t1].bitcast(FP8X4), scales=y_sc[:, t0:t1], in_=yt[:, PACK * t0 : PACK * t1])
            if t1 in CODE_STORES:
                s0 = ([0] + CODE_STORES)[CODE_STORES.index(t1)]
                nc.sync.dma_start(
                    out=out_1[0].rearrange("p m t -> p (m t)").bitcast(I32)[:, s0:t1],
                    in_=y_w[:, PACK * s0 : PACK * t1].bitcast(I32),
                )
            if t1 in SCALE_STORES:
                s0 = ([0] + SCALE_STORES)[SCALE_STORES.index(t1)]
                for q in range(4):
                    queue = nc.scalar if t1 == T and q % 2 == 0 else nc.sync
                    queue.dma_start(
                        out=out_2[0, q:16:4, s0:t1].bitcast(I32),
                        in_=y_sc[q:P:32, s0:t1].bitcast(I32),
                    )

        half = PART // 2
        before_gain = {}
        late_steps = {6: [(interleave_p, (2, 0, PART))]}
        lead_steps = {
            0: [(copy_gains, ())],
            1: [(interleave_lead, (0, "gpsimd", 0, 3 * S // 4))],
            2: [(interleave_lead, (0, "scalar", 3 * S // 4, S)), (interleave_lead, (1, "vector", 0, S // 2))],
            3: [(interleave_lead, (1, "scalar", S // 2, 3 * S // 4)), (quantize_lead, (0,)), (quantize_p, (0, 0))],
            4: [(interleave_lead, (1, "scalar", 3 * S // 4, S)), (quantize_lead, (1,)), (quantize_p, (1, 0)), (scale_bg, (15,))],
            6: [(scale_slots, (2, 0, 4))],
            11: [(widen_calib, ())],
            13: [(scale_bg, (14,))],
        }
        quantize_slot = {7: 2}
        wide = CHUNKS.count(PART)
        units = [(c, g) for g in range(FG) for c in range(2)] + [(c, g) for c in range(2, wide) for g in range(FG)]
        tile_slot = [max(j + STAGE2_LAG, FIRST_TILE_SLOT + 2 * j // 3) for j in range(TILES)]
        to_copy = []
        to_quantize = []
        rounded = 0
        turned = 0
        for slot, (c, g) in enumerate(units):
            tiles = [j for j in range(TILES) if tile_slot[j] == slot]
            stage1(c, g, 0)
            for step, args in before_gain.get(slot, []):
                step(*args)
            if slot > 0 and units[slot - 1] not in ON_SCALAR:
                scale_p(*units[slot - 1], 0)
            for step, args in lead_steps.get(slot, []):
                step(*args)
            whole = slot > FIRST_TILE_SLOT + 1 and units[slot - 1][1] == FG - 1 or slot in quantize_slot
            chunk = quantize_slot.get(slot, units[slot - 1][0])
            for j in tiles[:-1]:
                stage2(j, "turn" if j < 4 else "e_ps")
                if whole:
                    quantize_p(chunk, 0)
                calibrate(j)
            if to_copy:
                for pair in to_copy:
                    copy_turned(*pair)
                to_quantize.append((turned - 4, 4))
                to_copy = []
            elif tile_slot[rounded] + ROUND_LAG < slot < len(units) - 1:
                round_y(rounded)
                rounded += 1
            stage1(c, g, 1, *(("e_ps", 2) if 1 < slot < FIRST_TILE_SLOT - 1 else ()))
            for step, args in late_steps.get(slot, []):
                step(*args)
            if slot == len(units) - 1:
                continue
            for j in tiles[-1:]:
                stage2(j)
            if whole and len(tiles) < 2:
                quantize_p(chunk, 0)
            elif to_quantize and len(tiles) < 2:
                quantize_y(*to_quantize[0])
                to_quantize = to_quantize[1:]
            for j in tiles[-1:]:
                calibrate(j)
            if rounded - turned >= 4 and turned == 0:
                for first in (turned, turned + 2):
                    turn_y(first, 2)
                    to_copy.append((first, 2))
                turned += 4
            if tile_slot[rounded] + ROUND_LAG <= slot and slot < len(units) - 2:
                round_y(rounded)
                rounded += 1

        turn_y(4, 2)
        turn_y(6, 2)
        copy_turned(4, 2)
        copy_turned(6, 2)
        scale_p(6, 1, 0)
        stage2(10)
        quantize_p(6, 0)
        quantize_y(4, 4)
        calibrate(10)
        stage1(7, 0, 0)
        for j in range(rounded, 10):
            round_y(j)
        stage1(7, 1, 0)
        scale_p(7, 0, 0)
        stage2(11)
        calibrate(11)
        scale_p(7, 1, 0)
        stage1(8, 0, 0)
        scale_p(8, 0, 0)
        stage2(12)
        quantize_p(7, 0)
        calibrate(12)
        stage1(8, 1, 0)
        round_y(10)
        scale_p(8, 1, 0)
        stage2(13)
        quantize_p(8, 0)
        round_y(11)
        spread_calib()
        turn_y(8, 2)
        copy_turned(8, 2)
        stage2(14, "u_ps", 3)
        round_on_vector(13)
        calibrate(13)
        turn_y(10, 2)
        stage2(15, "u_ps", 3)
        round_y(12)
        copy_turned(10, 2)
        turn_terms(14)
        turn_y(12, 2)
        turn_terms(15)
        round_turned(14)
        copy_turned(12, 2)
        round_turned(15)
        add_scaled(14)
        add_scaled(15)
        quantize_y(8, 4)
        quantize_y(12, 3)
        quantize_y(15, 1)
